import numpy as np, ml_dtypes
CORES = [19,27,51,107,147,155,179,235,275,283,307,363,403,411,435,491]
N = 16
T, EL, CAP, CAPP = 1024, 4, 240, 64
E = N * EL
def entries(a): return a.T.reshape(-1)
def pack(v, P): return np.ascontiguousarray(np.asarray(v, np.int32).reshape(-1, P).T)
def lists(rng, how):
    if how == "uniform": return {"ex": np.stack([pack(rng.permutation(np.repeat(np.arange(E), CAPP))[:T], 16) for r in range(N)])}
    R = np.arange(N)[:, None]; c = rng.permutation(E); C = np.zeros((N, E), np.int64)
    if how == "bands":
        a = c % N; C = CAPP * ((R >= a) & (R <= a + CAP // CAPP)); C[a, np.arange(E)] = np.where(c < N, CAPP, rng.integers(1, CAPP + 1, E))
    if how == "full":
        g = T // CAPP; C[:, c[:g]] = CAPP; C[:, c[:g // 2]] = rng.integers(CAPP // 2, CAPP + 1, (N, g // 2))
    if how in ("skew", "sorted"):
        V = np.full((N, 3), CAP // N); V[:, 0] = rng.integers(2, CAP // N + 1, N); h = rng.integers(1, N - 2); V[h, 0] = 0; V[h + 1, 0] = 1; V[rng.integers(N), 1:] += CAP % N; V[rng.integers(N), 2] += 1
        W = rng.random((N, E)) ** 4 + 1e-9; W[:, c[:3]] = 0
        C = np.minimum(((T - T // 8 - V.sum(axis=1, keepdims=True)) * W / W.sum(axis=1, keepdims=True)).astype(np.int64), CAPP); C[:, c[:3]] = V
    if how == "thin":
        C = rng.integers(0, CAP // N + 1, (N, E)); C[1] = 1; C[[0, N // 2, N - 1]] = 0
    X = np.stack([rng.permutation(np.concatenate([np.repeat(np.arange(E), C[r]), np.full(T - C[r].sum(), -1)])) for r in range(N)])
    if how == "sorted": X = np.sort(X, axis=1); X[1::2] = X[1::2, ::-1].copy()
    return {"ex": np.stack([pack(v, 16) for v in X])}
def blank(d):
    for r in range(0, N, 2):
        u, i = np.unique(entries(d["ex"][r])[::-1], return_index=True); d["x"][r][:, T - 1 - i[u >= 0]] = 0
def setup_inputs(rng):
    return dict({"x": rng.standard_normal((N, 128, T), dtype=np.float32).astype(ml_dtypes.bfloat16)}, **lists(rng, "uniform"))
def setup_inputs_bands(rng):
    d = setup_inputs(rng); d.update(lists(rng, "bands"))
    for k in ("x",): d[k] = (d[k].astype(np.float32) * 1048576.0).astype(d[k].dtype)
    blank(d)
    return d
def setup_inputs_full(rng):
    d = setup_inputs(rng); d.update(lists(rng, "full"))
    for k in ("x",): d[k] = (d[k].astype(np.float32) * (1 / 1024.0)).astype(d[k].dtype)
    blank(d)
    return d
def setup_inputs_skew(rng):
    d = setup_inputs(rng); d.update(lists(rng, "skew"))
    blank(d)
    return d
def setup_inputs_sorted(rng):
    d = setup_inputs(rng); d.update(lists(rng, "sorted"))
    blank(d)
    return d
def setup_inputs_thin(rng):
    d = setup_inputs(rng); d.update(lists(rng, "thin"))
    blank(d)
    return d
def check_inputs(x):
    bad = []
    if x["ex"].min() < -1 or x["ex"].max() >= E: bad.append("ex out of range")
    if max(int(np.bincount(entries(a)[entries(a) >= 0], minlength=E).max()) for a in x["ex"]) > CAPP: bad.append("more than CAPP tokens of one rank choose one expert")
    return bad
def reference(x, ex):
    X = np.concatenate(list(x), axis=1); e = np.concatenate([entries(a) for a in ex])
    k = np.nonzero(e >= 0)[0]; o = k[np.argsort(e[k], kind="stable")]; s = e[o]
    p = np.arange(len(o)) - np.searchsorted(s, s)
    Y = np.zeros((128, E * CAP), x.dtype); m = p < CAP; Y[:, CAP * s[m] + p[m]] = X[:, o[m]]
    return {"y": np.stack([Y[:, EL * CAP * r:EL * CAP * (r + 1)] for r in range(N)])}

@@ -1,0 +1,489 @@
+from concourse.bass import DstId, RemoteDMATransfer
+from concourse.mybir import AluOpType as Op, ActivationFunctionType as Act
+
+NC = 60
+BIN0 = 1024
+BW = 256
+PWZ, PWW = 2048, 2480
+FWW = 3440
+
+SCRATCH = {
+    "xs": ("sbuf", [128, 1024], "bfloat16"),
+    "exr": ("sbuf", [128, 64], "int32"),
+    "off": ("sbuf", [128, 64], "uint16"),
+    "bins": ("sbuf", [128, 5120], "bfloat16"),
+    "craw": ("sbuf", [128, 128], "bfloat16"),
+    "pw": ("sbuf", [128, PWW], "bfloat16"),
+    "fw": ("sbuf", [128, FWW], "bfloat16"),
+    "pk": ("sbuf", [128, 960], "bfloat16"),
+    "yt": ("sbuf", [128, 960], "bfloat16"),
+    "zz": ("sbuf", [128, 512], "bfloat16"),
+    "ones": ("sbuf", [128, 128], "bfloat16"),
+    "nones": ("sbuf", [128, 128], "bfloat16"),
+    "rst": ("sbuf", [128, 512], "bfloat16"),
+    "am": ("sbuf", [128, 128], "int32"),
+    "am4": ("sbuf", [128, 128], "int32"),
+    "am15": ("sbuf", [128, 128], "int32"),
+    "v8": ("sbuf", [128, 8], "int32"),
+    "eci": ("sbuf", [128, 8], "int32"),
+    "ecol": ("sbuf", [128, 8], "float32"),
+    "wcol": ("sbuf", [128, 8], "float32"),
+    "icol": ("sbuf", [128, 3], "int32"),
+    "fcol": ("sbuf", [128, 4], "float32"),
+    "sameg": ("sbuf", [128, 128], "bfloat16"),
+    "sm": ("sbuf", [128, 128], "bfloat16"),
+    "nba": ("sbuf", [128, 128], "bfloat16"),
+    "nb": ("sbuf", [128, 128], "bfloat16"),
+    "idm": ("sbuf", [128, 128], "bfloat16"),
+    "id256": ("sbuf", [128, 128], "bfloat16"),
+    "nid": ("sbuf", [128, 128], "bfloat16"),
+    "c2": ("sbuf", [128, 64], "bfloat16"),
+    "p16": ("sbuf", [128, NC], "bfloat16"),
+    "pc": ("sbuf", [128, NC], "bfloat16"),
+    "k0": ("sbuf", [128, NC], "bfloat16"),
+    "k1": ("sbuf", [128, NC], "bfloat16"),
+    "xt": ("sbuf", [128, NC], "bfloat16"),
+    "mxa": ("sbuf", [128, NC], "bfloat16"),
+    "mx0": ("sbuf", [128, NC], "bfloat16"),
+    "mx1": ("sbuf", [128, NC], "bfloat16"),
+    "c248": ("sbuf", [128, 16], "float32"),
+    "oh": ("sbuf", [128, 512], "bfloat16"),
+    "ohw": ("sbuf", [128, 512], "bfloat16"),
+    "inc": ("sbuf", [128, 512], "bfloat16"),
+    "pr": ("sbuf", [128, 512], "bfloat16"),
+    "nt": ("sbuf", [128, 192], "bfloat16"),
+    "cum": ("sbuf", [128, 24], "float32"),
+    "rb0": ("sbuf", [128, 9 * NC], "bfloat16"),
+    "rb1": ("sbuf", [128, 9 * NC], "bfloat16"),
+    "ind": ("sbuf", [128, 16 * NC], "bfloat16"),
+    "ic": ("sbuf", [128, 16 * NC], "bfloat16"),
+    "indt": ("sbuf", [128, NC], "bfloat16"),
+    "ix": ("sbuf", [128, NC], "bfloat16"),
+    "ib": ("sbuf", [128, NC], "bfloat16"),
+    "offp": ("sbuf", [128, NC], "uint16"),
+    "offf": ("sbuf", [128, NC], "uint16"),
+    "pl0": ("psum", [128, 512], "float32"),
+    "pl1": ("psum", [128, 512], "float32"),
+    "pslot": ("psum", [128, 512], "float32"),
+    "pb": ("psum", [128, 512], "float32"),
+    "pcn": ("psum", [128, 512], "float32"),
+    "pbt": ("psum", [128, 512], "float32"),
+    "po0": ("psum", [128, 512], "float32"),
+    "po1": ("psum", [128, 512], "float32"),
+}
+SEMAPHORES = ["sv", "st", "ss", "sg", "sex", "sx", "loc", "sxr", "offr", "cnt", "cntf", "twd", "own", "pkd", "sy"]
+
+_memo = {}
+
+
+def _bits(mask):
+    return [b for b in range(16) if mask >> b & 1]
+
+
+def _halves(mask):
+    b = _bits(mask)
+    h = len(b) // 2
+    return sum(1 << k for k in b[:h]), sum(1 << k for k in b[h:])
+
+
+def _plan(cores, topo):
+    if "plan" in _memo:
+        return _memo["plan"]
+    n = len(cores)
+    plan = []
+    for r in range(n):
+        c = cores[r]
+        rack = [q for q in range(n) if topo.rack(topo.host(cores[q])) == topo.rack(topo.host(c))]
+        other = [q for q in range(n) if q not in rack]
+        twin = [q for q in other if topo.chip(cores[q]) == topo.chip(c) and topo.may_write(c, cores[q])][0]
+        i = rack.index(r)
+        peers = [rack[(i + d) % len(rack)] for d in range(1, len(rack))]
+        same = [q for q in peers if topo.same_plane(c, cores[q])]
+        cross = [q for q in peers if q not in same]
+        base = c - c % topo.CORES_PER_CHIP
+        help_ = [h for h in range(base, base + topo.CORES_PER_CHIP)
+                 if topo.die(h) != topo.die(c) and all(topo.may_write(h, cores[q]) for q in peers)]
+        sends = [(c, [cross[0], cross[2], same[0]]), (help_[0], [cross[1], same[1]]), (help_[1], [cross[3], same[2]])]
+        plan.append({"rack": rack, "other": other, "twin": twin, "i": i, "sends": sends})
+    _memo["plan"] = plan
+    return plan
+
+
+def _groups(dests, mask):
+    a, b = _halves(mask)
+    out = [[(dests[0], a), (dests[1], b)]]
+    if len(dests) == 3:
+        out.append([(dests[2], mask)])
+    return out
+
+
+def _arrivals(plan, cores, topo, r):
+    tot = cn = 0
+    for s in plan[r]["rack"]:
+        for c, dests in plan[s]["sends"]:
+            if r in dests:
+                m = topo.mask(c, cores[r])
+                cn += len(_bits(m))
+                for grp in _groups(dests, m):
+                    for q, mm in grp:
+                        if q == r:
+                            tot += len(_bits(mm))
+    return tot, cn
+
+
+def _dst(topo, d, c):
+    rid, pid = topo.addr(d, c)
+    return DstId(rid=rid, pnc=pid)
+
+
+def _multi(g, topo, core, dests, ap, mask, sem, loc):
+    g.remote_dma_fused([RemoteDMATransfer(dst_ids=[_dst(topo, d, core) for d in dests], dma_engine_mask=mask, remote_sem=sem,
+                                          srcs=[ap], dsts=[ap for d in dests])], local_sem=loc)
+    return len(_bits(mask))
+
+
+def _send_bins(g, T, topo, core, plan, src, dests, twins):
+    mask = topo.mask(core, T.cores[dests[0]])
+    i = plan[src]["i"]
+    first = plan[src]["rack"][0] < plan[src]["other"][0]
+    fo = 0 if first else 960
+    done = 0
+    for grp in _groups(dests, mask):
+        trs = []
+        for q, m in grp:
+            e = plan[q]["twin"] if twins else q
+            s = T.bins[:, BIN0 + BW * e:BIN0 + BW * e + BW]
+            d = T.pw[:, BW * i:BW * i + BW] if twins else T.fw[:, fo + BW * i:fo + BW * i + BW]
+            trs.append(RemoteDMATransfer(dst_ids=[_dst(topo, T.cores[q], core)], dma_engine_mask=m,
+                                         remote_sem=T.sem.twd if twins else T.sem.own, srcs=[s], dsts=[d]))
+            done += len(_bits(m))
+        g.remote_dma_fused(trs, local_sem=T.sem.loc)
+    return done
+
+
+def _fill_ranges(plan, dests, own):
+    b = sorted(set(dests + [plan[q]["twin"] for q in dests] + own))
+    runs = []
+    for k in b:
+        if runs and runs[-1][1] == k and k - runs[-1][0] < 2:
+            runs[-1][1] = k + 1
+        else:
+            runs.append([k, k + 1])
+    return [(BIN0 + BW * a, BIN0 + BW * z) for a, z in runs]
+
+
+def rank_program(g, core, T, topo):
+    plan = _plan(T.cores, topo)
+    rank = T.rank_of(core)
+    if rank is not None:
+        _rank(g, core, rank, T, topo, plan)
+        return
+    for r in range(len(plan)):
+        for c, dests in plan[r]["sends"]:
+            if c == core:
+                _helper(g, core, r, dests, T, topo, plan)
+
+
+def _helper(g, core, r, dests, T, topo, plan):
+    rc = T.cores[r]
+    onchip = topo.mask(rc, core)
+    offchip = topo.mask(core, T.cores[dests[0]])
+    i = plan[r]["i"]
+    nv = 0
+    for a, z in _fill_ranges(plan, dests, []):
+        g.vector.memset(T.bins[:, a:z], 0.0).then_inc(T.sem.sv, 1)
+        nv += 1
+    slot = T.craw[:, 64 + 8 * i:72 + 8 * i]
+    g.wait_ge(T.sem.cnt, len(_bits(topo.mask(rc, T.cores[plan[r]["sends"][0][1][0]]))))
+    loc = _multi(g, topo, core, [T.cores[q] for q in dests], slot, offchip, T.sem.cnt, T.sem.loc)
+    g.vector.wait_ge(T.sem.sv, nv)
+    g.vector.wait_ge(T.sem.sxr, len(_bits(onchip)))
+    g.vector.wait_ge(T.sem.offr, len(_bits(onchip & ~offchip)))
+    g.vector.tensor_copy(T.bins[:, 0:5120].indirect(T.off[:, 0:64]), T.xs[:, :]).then_inc(T.sem.sv, 1)
+    nv += 1
+    g.wait_ge(T.sem.sv, nv)
+    loc += _send_bins(g, T, topo, core, plan, r, dests, True)
+    loc += _send_bins(g, T, topo, core, plan, r, dests, False)
+    g.wait_ge(T.sem.loc, loc)
+
+
+def _rank(g, core, r, T, topo, plan):
+    P = plan[r]
+    i, rack, twin = P["i"], P["rack"], P["twin"]
+    first = rack[0] < P["other"][0]
+    dests = P["sends"][0][1]
+    helpers = [c for c, d in P["sends"][1:]]
+    onchip = topo.mask(core, helpers[0])
+    offchip = topo.mask(core, T.cores[dests[0]])
+    inner = onchip & ~offchip
+    tot, cn = _arrivals(plan, T.cores, topo, r)
+
+    Q = {"v": g.vector, "t": g.tensor, "s": g.scalar, "g": g, "y": g.sync}
+    S = {"v": T.sem.sv, "t": T.sem.st, "s": T.sem.ss, "g": T.sem.sg}
+    n = {"v": 0, "t": 0, "s": 0, "g": 0}
+    seen = {}
+
+    def did(q, ins):
+        ins.then_inc(S[q], 1)
+        n[q] += 1
+        return (q, n[q])
+
+    def need(q, *toks):
+        for src, k in toks:
+            if seen.get((q, src), 0) < k:
+                Q[q].wait_ge(S[src], k)
+                seen[(q, src)] = k
+
+    def ts(out, in0, s1, op, s2=None, op1=None):
+        if op1 is None:
+            return did("v", g.vector.tensor_scalar(out, in0, s1, None, op))
+        return did("v", g.vector.tensor_scalar(out, in0, s1, s2, op, op1))
+
+    def tt(out, a, b, op):
+        return did("v", g.vector.tensor_tensor(out, a, b, op))
+
+    def cp(out, a):
+        return did("v", g.vector.tensor_copy(out, a))
+
+    def fill(ap, v):
+        return did("v", g.vector.memset(ap, v))
+
+    def act(out, in_, **kw):
+        return did("s", g.scalar.activation(out, in_, Act.Copy, **kw))
+
+    def mm(out, l, rh, start, stop):
+        return did("t", g.tensor.matmul(out, l, rh, start, stop))
+
+    for a in range(8):
+        q = g.sync if a % 2 == 0 else g.scalar
+        q.dma_start(T.exr[16 * a:16 * a + 16, :], T.ex[:, :]).then_inc(T.sem.sex, 16)
+    g.sync.dma_start(T.xs[:, :], T.x[:, :]).then_inc(T.sem.sx, 16)
+
+    pi, gi, qi = T.icol[:, 0:1], T.icol[:, 1:2], T.icol[:, 2:3]
+    pf, gcol, qcol, q8 = T.fcol[:, 0:1], T.fcol[:, 1:2], T.fcol[:, 2:3], T.fcol[:, 3:4]
+    did("g", g.iota(T.am[:, :], [[1, 128]], 0, 0))
+    did("g", g.iota(T.v8[:, :], [[128, 8]], 0, 1))
+    G_pi = did("g", g.iota(pi, [[0, 1]], 0, 1))
+    fl = {"allow_small_or_imprecise_dtypes": True}
+    G_c2 = did("g", g.iota(T.c2[:, :], [[2, 64]], 0, 0, **fl))
+    G_p16 = did("g", g.iota(T.p16[:, :], [[0, 4], [16, 15]], 0, 0, **fl))
+    did("g", g.iota(T.k0[:, :], [[64, 4], [16, 15]], 0, 0, **fl))
+    if first:
+        G_xt = did("g", g.iota(T.xt[:, :], [[176, 4], [0, 15]], 0, 0, **fl))
+        k1 = T.k0
+    else:
+        did("g", g.iota(T.k1[:, :], [[240, 4], [16, 15]], 0, 0, **fl))
+        G_xt = did("g", g.iota(T.xt[:, :], [[-176, 4], [0, 15]], 960, 0, **fl))
+        k1 = T.k1
+
+    z0 = fill(T.zz[:, :], 0.0)
+    V_ones = fill(T.ones[:, :], 1.0)
+    t = fill(T.rst[:, :], 1.0)
+
+    mx = {}
+    need("g", V_ones)
+    G_mx = None
+    for half in sorted(set([r % 2, twin % 2])):
+        m = T.mx0 if half == 0 else T.mx1
+        g0 = 4 * half
+        if G_mx is not None:
+            need("g", G_mx)
+        a = did("g", g.affine_select(T.mxa[:, :], T.ones[:, 0:NC], [[-16, 4], [0, 15]], Op.is_ge, 0.0, -16 * g0, 1))
+        need("g", a)
+        G_mx = did("g", g.affine_select(m[:, :], T.mxa[:, :], [[16, 4], [0, 15]], Op.is_ge, 0.0, 16 * g0 + 15, -1))
+        mx[half] = m
+
+    need("v", t)
+    fill(T.rst[:, 0::64], 0.0)
+    need("v", G_pi)
+    ts(gi, pi, 4, Op.arith_shift_right)
+    ts(qi, pi, 15, Op.bitwise_and)
+    cp(pf, pi)
+    ts(T.am4[:, :], T.am[:, :], 4, Op.arith_shift_right)
+    ts(T.am15[:, :], T.am[:, :], 15, Op.bitwise_and)
+    t = ts(T.eci[:, :], T.v8[:, :], 4, Op.arith_shift_right)
+    need("v", t)
+    cp(T.ecol[:, :], T.eci[:, :])
+    V_w = ts(T.wcol[:, :], T.eci[:, :], 64.0, Op.mult, float(BIN0), Op.add)
+    cp(gcol, gi)
+    V_q = cp(qcol, qi)
+    ts(q8, qi, 0.125, Op.mult)
+    t = ts(T.nba[:, :], T.am[:, :], pf, Op.is_le, -1.0, Op.mult)
+    need("v", V_q)
+    ts(T.sm[:, :], T.am15[:, :], qcol, Op.is_equal)
+    t = ts(T.sameg[:, :], T.am4[:, :], gcol, Op.is_equal)
+    need("v", t)
+    tt(T.nb[:, :], T.nba[:, :], T.sameg[:, :], Op.mult)
+
+    need("s", z0)
+    for a, z in _fill_ranges(plan, dests, [r, twin]):
+        S_fill = act(T.bins[:, a:z], T.zz[:, 0:z - a])
+
+    g.vector.wait_ge(T.sem.sex, 128)
+    V_oh = []
+    for k in range(8):
+        V_oh.append(ts(T.oh[:, 64 * k:64 * k + 64], T.exr[:, :], T.ecol[:, k:k + 1], Op.is_equal))
+    V_scan = []
+    need("v", V_oh[7])
+    for h in range(2):
+        w = slice(256 * h, 256 * h + 256)
+        V_scan.append(did("v", g.vector.tensor_tensor_scan(T.inc[:, w], T.rst[:, w], T.oh[:, w], 0.0, Op.mult, Op.add)))
+    for k in range(8):
+        need("s", V_oh[k], V_w)
+        S_ohw = act(T.ohw[:, 64 * k:64 * k + 64], T.oh[:, 64 * k:64 * k + 64], scale=T.wcol[:, k:k + 1])
+    need("t", V_oh[7])
+    T_pl = []
+    mm(T.pl0[:, 0:256], T.nb[:, :], T.oh[:, 0:256], True, False)
+    mm(T.pl1[:, 0:256], T.nb[:, :], T.oh[:, 256:512], True, False)
+    for h in range(2):
+        need("t", V_scan[h])
+        T_pl.append(mm((T.pl0 if h == 0 else T.pl1)[:, 0:256], T.sameg[:, :], T.inc[:, 256 * h:256 * h + 256], False, True))
+    need("v", V_scan[1])
+    V_cnt = cp(T.craw[:, 64 + 8 * i:72 + 8 * i], T.inc[:, 63::64])
+    n0, n1, n2 = T.nt[:, 0:64], T.nt[:, 64:128], T.nt[:, 128:192]
+    ts(n1, T.exr[:, :], 0.0, Op.is_lt, q8, Op.mult)
+    t = ts(n0, T.exr[:, :], 0.0, Op.is_lt)
+    need("v", t, G_c2)
+    V_n = tt(n2, n0, T.c2[:, :], Op.mult)
+    V_pr = []
+    for h in range(2):
+        need("v", T_pl[h])
+        w = slice(256 * h, 256 * h + 256)
+        V_pr.append(tt(T.pr[:, w], (T.pl0 if h == 0 else T.pl1)[:, 0:256], T.oh[:, w], Op.mult))
+    sl = T.pslot[:, 0:64]
+    need("t", S_ohw)
+    for k in range(8):
+        mm(sl, T.sm[:, :], T.ohw[:, 64 * k:64 * k + 64], k == 0, False)
+    need("t", V_n)
+    mm(sl, T.sm[:, :], n1, False, False)
+    mm(sl, T.sm[:, :], n2, False, False)
+    for k in range(8):
+        need("t", V_pr[k // 4])
+        T_sl = mm(sl, T.sm[:, :], T.pr[:, 64 * k:64 * k + 64], False, k == 7)
+    need("v", T_sl)
+    V_off = cp(T.off[:, :], sl)
+    need("v", V_off, S_fill)
+    g.vector.wait_ge(T.sem.sx, 16)
+    V_sc = cp(T.bins[:, 0:5120].indirect(T.off[:, 0:64]), T.xs[:, :])
+
+    g.wait_ge(T.sem.sx, 16)
+    loc = _multi(g, topo, core, helpers, T.xs[:, :], onchip, T.sem.sxr, T.sem.loc)
+    need("g", V_cnt)
+    loc += _multi(g, topo, core, helpers + [T.cores[q] for q in dests], T.craw[:, 64 + 8 * i:72 + 8 * i], offchip,
+                  T.sem.cnt, T.sem.loc)
+    need("g", V_off)
+    loc += _multi(g, topo, core, helpers, T.off[:, :], inner, T.sem.offr, T.sem.loc)
+    need("g", V_sc)
+    loc += _send_bins(g, T, topo, core, plan, r, dests, True)
+    loc += _send_bins(g, T, topo, core, plan, r, dests, False)
+    if first:
+        g.wait_ge(T.sem.cnt, cn)
+        rid, pid = topo.addr(T.cores[twin], core)
+        g.remote_dma(T.craw[:, 0:64], T.craw[:, 64:128], T.sem.cntf, T.sem.loc, pid, rid, offchip)
+        loc += len(_bits(offchip))
+
+    fo, ptw = (0, 2048) if first else (960, 0)
+    need("s", V_sc)
+    act(T.pw[:, BW * i:BW * i + BW], T.bins[:, BIN0 + BW * twin:BIN0 + BW * twin + BW])
+    S_own = act(T.fw[:, fo + BW * i:fo + BW * i + BW], T.bins[:, BIN0 + BW * r:BIN0 + BW * r + BW])
+
+    ts(T.idm[:, :], T.am[:, :], pf, Op.is_equal)
+    ts(T.id256[:, :], T.am[:, :], pf, Op.is_equal, 256.0, Op.mult)
+    fill(T.nones[:, :], -1.0)
+    fill(T.c248[:, :], 248.0)
+    fill(T.rb0[:, 0:NC], 0.0)
+    if first:
+        fill(T.rb1[:, 0:NC], 0.0)
+    else:
+        ts(T.nid[:, :], T.am[:, :], pf, Op.is_equal, -1.0, Op.mult)
+        fill(T.fw[:, 960 + 2048:FWW], 0.0)
+    fill(T.pw[:, PWZ:PWW], 0.0)
+    need("v", G_mx, G_p16)
+    t = ts(T.pc[:, :], T.p16[:, :], qcol, Op.add)
+    need("v", t)
+
+    def listing(u, owner, kk, before):
+        col = owner // 2
+        m = mx[owner % 2]
+        rb, po, out = (T.rb0, T.po0, T.offp) if u == 0 else (T.rb1, T.po1, T.offf)
+        ind, ic = T.ind[:, 8 * NC * u:8 * NC * u + 8 * NC], T.ic[:, 8 * NC * u:8 * NC * u + 8 * NC]
+        io, w = 8 * NC * u, 8 * NC
+        lo, ns = (0, 16) if before else (64, 8)
+        cb = 0 if u == 0 else 8
+        t = did("v", g.vector.tensor_tensor_scan(T.cum[:, cb:cb + ns], T.craw[:, lo + col::8], T.c248[:, 0:ns], 0.0,
+                                                 Op.add, Op.min))
+        need("v", t)
+        if before:
+            ts(rb[:, 0:NC], m[:, :], T.cum[:, cb + 7:cb + 8], Op.mult)
+            cb += 8
+        for s in range(8):
+            t = ts(rb[:, NC * (s + 1):NC * (s + 2)], m[:, :], T.cum[:, cb + s:cb + s + 1], Op.mult)
+        need("t", t)
+        if before:
+            mm(T.pbt[:, 0:NC], T.ones[:, :], rb[:, 0:NC], True, True)
+        t_b = mm(T.pb[:, 0:w], T.ones[:, :], rb[:, NC:9 * NC], True, True)
+        mm(T.pcn[:, 0:w], T.nones[:, :], rb[:, NC:9 * NC], True, False)
+        t_c = mm(T.pcn[:, 0:w], T.ones[:, :], rb[:, 0:w], False, True)
+        need("v", t_b)
+        if before:
+            tt(T.indt[:, :], T.pc[:, :], T.pbt[:, 0:NC], Op.is_ge)
+        for s in range(8):
+            v_i = tt(T.ind[:, io + NC * s:io + NC * s + NC], T.pc[:, :], T.pb[:, NC * s:NC * s + NC], Op.is_ge)
+        need("v", t_c, v_i)
+        v_c = tt(ic, ind, T.pcn[:, 0:w], Op.mult)
+        extra = []
+        if u == 1:
+            need("v", G_xt)
+            v_c = tt(T.ix[:, :], T.indt[:, :] if before else T.ind[:, io + NC * 7:io + NC * 8], T.xt[:, :], Op.mult)
+            extra.append((T.idm, T.ix))
+            if before:
+                v_c = tt(T.ib[:, :], T.indt[:, :], T.pbt[:, 0:NC], Op.mult)
+                extra.append((T.nid, T.ib))
+        o = po[:, 0:NC]
+        need("t", G_xt, v_i)
+        mm(o, T.idm[:, :], kk[:, :], True, False)
+        for s in range(8):
+            mm(o, T.id256[:, :], T.ind[:, io + NC * s:io + NC * s + NC], False, False)
+        need("t", v_c)
+        for l, rh in extra:
+            mm(o, l[:, :], rh[:, :], False, False)
+        for s in range(8):
+            t = mm(o, T.idm[:, :], T.ic[:, io + NC * s:io + NC * s + NC], False, s == 7)
+        need("v", t)
+        return ts(out[:, :], o, qcol, Op.add)
+
+    g.vector.wait_ge(T.sem.cnt, cn)
+    V_lp = listing(0, twin, T.k0, False)
+    need("v", V_lp, S_own)
+    need("s", V_lp, S_own)
+    g.vector.wait_ge(T.sem.twd, tot)
+    V_pk = cp(T.pk[:, 0:480], T.pw[:, :].indirect(T.offp[:, 0:30]))
+    g.scalar.wait_ge(T.sem.twd, tot)
+    S_pk = act(T.pk[:, 480:960], T.pw[:, :].indirect(T.offp[:, 30:60]))
+    need("g", V_pk, S_pk)
+    tp = 0 if first else 2048
+    rid, pid = topo.addr(T.cores[twin], core)
+    g.remote_dma(T.fw[:, tp:tp + 960], T.pk[:, :], T.sem.pkd, T.sem.loc, pid, rid, offchip)
+    loc += len(_bits(offchip))
+
+    npk = len(_bits(topo.mask(T.cores[twin], core)))
+    if not first:
+        g.vector.wait_ge(T.sem.cntf, npk)
+    V_lf = listing(1, r, k1, not first)
+    need("v", V_lf)
+    need("s", V_lf)
+    fe = 3008 if first else FWW
+    for q in (g.vector, g.scalar):
+        q.wait_ge(T.sem.own, tot)
+        q.wait_ge(T.sem.pkd, npk)
+    V_y = cp(T.yt[:, 0:480], T.fw[:, 0:fe].indirect(T.offf[:, 0:30]))
+    S_y = act(T.yt[:, 480:960], T.fw[:, 0:fe].indirect(T.offf[:, 30:60]))
+    need("y", V_y)
+    g.sync.dma_start(T.y[:, 0:480], T.yt[:, 0:480]).then_inc(T.sem.sy, 16)
+    need("s", S_y)
+    g.scalar.dma_start(T.y[:, 480:960], T.yt[:, 480:960]).then_inc(T.sem.sy, 16)
+
+    g.wait_ge(T.sem.loc, loc)
+    for q in ("v", "t", "s", "g"):
+        need("g", (q, n[q]))
+    g.wait_ge(T.sem.sy, 32)

@@ -1,77 +1,74 @@
 from concourse.bass import DstId, RemoteDMATransfer
-from concourse.mybir import AluOpType as Op, ActivationFunctionType as Act
+from concourse.mybir import AluOpType as Op, ActivationFunctionType as Act, AxisListType as Ax
 
-NC = 60
-BIN0 = 1024
+EL = 4
 BW = 256
-PWZ, PWW = 2048, 2480
-FWW = 3440
+NE = 32
+ZC = 4096
+FWW = ZC + 432
+NM = 15
 
 SCRATCH = {
     "xs": ("sbuf", [128, 1024], "bfloat16"),
-    "exr": ("sbuf", [128, 64], "int32"),
-    "off": ("sbuf", [128, 64], "uint16"),
-    "bins": ("sbuf", [128, 5120], "bfloat16"),
-    "craw": ("sbuf", [128, 128], "bfloat16"),
-    "pw": ("sbuf", [128, PWW], "bfloat16"),
+    "exc": ("sbuf", [128, 8], "int32"),
+    "bins": ("sbuf", [128, 2048], "bfloat16"),
     "fw": ("sbuf", [128, FWW], "bfloat16"),
-    "pk": ("sbuf", [128, 960], "bfloat16"),
     "yt": ("sbuf", [128, 960], "bfloat16"),
-    "zz": ("sbuf", [128, 512], "bfloat16"),
-    "ones": ("sbuf", [128, 128], "bfloat16"),
-    "nones": ("sbuf", [128, 128], "bfloat16"),
-    "rst": ("sbuf", [128, 512], "bfloat16"),
-    "am": ("sbuf", [128, 128], "int32"),
-    "am4": ("sbuf", [128, 128], "int32"),
-    "am15": ("sbuf", [128, 128], "int32"),
-    "v8": ("sbuf", [128, 8], "int32"),
-    "eci": ("sbuf", [128, 8], "int32"),
-    "ecol": ("sbuf", [128, 8], "float32"),
-    "wcol": ("sbuf", [128, 8], "float32"),
-    "icol": ("sbuf", [128, 3], "int32"),
-    "fcol": ("sbuf", [128, 4], "float32"),
-    "sameg": ("sbuf", [128, 128], "bfloat16"),
-    "sm": ("sbuf", [128, 128], "bfloat16"),
-    "nba": ("sbuf", [128, 128], "bfloat16"),
-    "nb": ("sbuf", [128, 128], "bfloat16"),
+    "craw": ("sbuf", [128, 16 * NE], "bfloat16"),
+    "pi": ("sbuf", [128, 8], "int32"),
+    "ai": ("sbuf", [128, 8], "int32"),
+    "qi": ("sbuf", [128, 8], "int32"),
+    "gi": ("sbuf", [128, 8], "int32"),
+    "ri": ("sbuf", [128, 8], "int32"),
+    "fcol": ("sbuf", [128, 8], "float32"),
+    "prow": ("sbuf", [128, 128], "bfloat16"),
+    "arow": ("sbuf", [128, 128], "bfloat16"),
+    "qrow": ("sbuf", [128, 128], "bfloat16"),
+    "grow": ("sbuf", [128, 64], "bfloat16"),
+    "hrow": ("sbuf", [128, 8], "float32"),
+    "colid": ("sbuf", [128, 8], "float32"),
+    "rst": ("sbuf", [128, 256], "bfloat16"),
+    "ones": ("sbuf", [128, 8], "bfloat16"),
+    "samea": ("sbuf", [128, 128], "bfloat16"),
+    "blt": ("sbuf", [128, 128], "bfloat16"),
+    "dn0": ("sbuf", [128, 128], "bfloat16"),
+    "dneg": ("sbuf", [128, 128], "bfloat16"),
     "idm": ("sbuf", [128, 128], "bfloat16"),
-    "id256": ("sbuf", [128, 128], "bfloat16"),
-    "nid": ("sbuf", [128, 128], "bfloat16"),
-    "c2": ("sbuf", [128, 64], "bfloat16"),
-    "p16": ("sbuf", [128, NC], "bfloat16"),
-    "pc": ("sbuf", [128, NC], "bfloat16"),
-    "k0": ("sbuf", [128, NC], "bfloat16"),
-    "k1": ("sbuf", [128, NC], "bfloat16"),
-    "xt": ("sbuf", [128, NC], "bfloat16"),
-    "mxa": ("sbuf", [128, NC], "bfloat16"),
-    "mx0": ("sbuf", [128, NC], "bfloat16"),
-    "mx1": ("sbuf", [128, NC], "bfloat16"),
-    "c248": ("sbuf", [128, 16], "float32"),
-    "oh": ("sbuf", [128, 512], "bfloat16"),
-    "ohw": ("sbuf", [128, 512], "bfloat16"),
-    "inc": ("sbuf", [128, 512], "bfloat16"),
-    "pr": ("sbuf", [128, 512], "bfloat16"),
-    "nt": ("sbuf", [128, 192], "bfloat16"),
-    "cum": ("sbuf", [128, 24], "float32"),
-    "rb0": ("sbuf", [128, 9 * NC], "bfloat16"),
-    "rb1": ("sbuf", [128, 9 * NC], "bfloat16"),
-    "ind": ("sbuf", [128, 16 * NC], "bfloat16"),
-    "ic": ("sbuf", [128, 16 * NC], "bfloat16"),
-    "indt": ("sbuf", [128, NC], "bfloat16"),
-    "ix": ("sbuf", [128, NC], "bfloat16"),
-    "ib": ("sbuf", [128, NC], "bfloat16"),
-    "offp": ("sbuf", [128, NC], "uint16"),
-    "offf": ("sbuf", [128, NC], "uint16"),
-    "pl0": ("psum", [128, 512], "float32"),
-    "pl1": ("psum", [128, 512], "float32"),
-    "pslot": ("psum", [128, 512], "float32"),
+    "tri0": ("sbuf", [128, 64], "bfloat16"),
+    "tri1": ("sbuf", [128, 64], "bfloat16"),
+    "tri": ("sbuf", [128, 64], "bfloat16"),
+    "sel": ("sbuf", [128, 8], "bfloat16"),
+    "kk": ("sbuf", [128, 60], "bfloat16"),
+    "kq": ("sbuf", [128, 60], "bfloat16"),
+    "nm": ("sbuf", [128, 16], "float32"),
+    "exf": ("sbuf", [128, 8], "float32"),
+    "ex4": ("sbuf", [128, 8], "float32"),
+    "oh": ("sbuf", [128, 256], "bfloat16"),
+    "inc": ("sbuf", [128, 256], "bfloat16"),
+    "pr": ("sbuf", [128, 256], "bfloat16"),
+    "junk": ("sbuf", [128, 256], "bfloat16"),
+    "plc": ("sbuf", [128, 8], "float32"),
+    "pli": ("sbuf", [128, 8], "int32"),
+    "mi": ("sbuf", [128, 8], "int32"),
+    "ki": ("sbuf", [128, 8], "int32"),
+    "kf": ("sbuf", [128, 8], "float32"),
+    "wf": ("sbuf", [128, 8], "float32"),
+    "lh": ("sbuf", [128, 1024], "float16"),
+    "rh": ("sbuf", [128, 1024], "float16"),
+    "off": ("sbuf", [128, 128], "uint16"),
+    "cc": ("sbuf", [128, 64], "bfloat16"),
+    "cb": ("sbuf", [128, 8], "bfloat16"),
+    "nc": ("sbuf", [128, 8], "float32"),
+    "bm": ("sbuf", [128, 16], "float32"),
+    "ind": ("sbuf", [128, NM * 128], "bfloat16"),
+    "offf": ("sbuf", [128, 60], "uint16"),
+    "pl": ("psum", [128, 512], "float32"),
+    "plist": ("psum", [128, 512], "float32"),
+    "pc": ("psum", [128, 512], "float32"),
     "pb": ("psum", [128, 512], "float32"),
-    "pcn": ("psum", [128, 512], "float32"),
-    "pbt": ("psum", [128, 512], "float32"),
-    "po0": ("psum", [128, 512], "float32"),
-    "po1": ("psum", [128, 512], "float32"),
+    "po": ("psum", [128, 512], "float32"),
 }
-SEMAPHORES = ["sv", "st", "ss", "sg", "sex", "sx", "loc", "sxr", "offr", "cnt", "cntf", "twd", "own", "pkd", "sy"]
+SEMAPHORES = ["sv", "st", "ss", "sg", "sex", "sx", "hex", "hx", "loc", "cnt", "bin", "sy"]
 
 _memo = {}
 
@@ -94,41 +91,38 @@ def _plan(cores, topo):
     for r in range(n):
         c = cores[r]
         rack = [q for q in range(n) if topo.rack(topo.host(cores[q])) == topo.rack(topo.host(c))]
-        other = [q for q in range(n) if q not in rack]
-        twin = [q for q in other if topo.chip(cores[q]) == topo.chip(c) and topo.may_write(c, cores[q])][0]
+        twin = [q for q in range(n) if q not in rack and topo.chip(cores[q]) == topo.chip(c) and topo.may_write(c, cores[q])][0]
         i = rack.index(r)
         peers = [rack[(i + d) % len(rack)] for d in range(1, len(rack))]
         same = [q for q in peers if topo.same_plane(c, cores[q])]
         cross = [q for q in peers if q not in same]
+        order = []
+        for k in range(max(len(same), len(cross))):
+            order += cross[k:k + 1] + same[k:k + 1]
         base = c - c % topo.CORES_PER_CHIP
-        help_ = [h for h in range(base, base + topo.CORES_PER_CHIP)
-                 if topo.die(h) != topo.die(c) and all(topo.may_write(h, cores[q]) for q in peers)]
-        sends = [(c, [cross[0], cross[2], same[0]]), (help_[0], [cross[1], same[1]]), (help_[1], [cross[3], same[2]])]
-        plan.append({"rack": rack, "other": other, "twin": twin, "i": i, "sends": sends})
+        proxy = [h for h in range(base, base + topo.CORES_PER_CHIP)
+                 if topo.die(h) != topo.die(c) and all(topo.may_write(h, cores[q]) for q in peers)][0]
+        plan.append({"rack": rack, "twin": twin, "order": order, "proxy": proxy})
     _memo["plan"] = plan
     return plan
 
 
-def _groups(dests, mask):
-    a, b = _halves(mask)
-    out = [[(dests[0], a), (dests[1], b)]]
-    if len(dests) == 3:
-        out.append([(dests[2], mask)])
-    return out
+def _sends(plan, r, proxy):
+    d = plan[r]["order"] + ([r] if proxy else [])
+    return [d[k:k + 2] for k in range(0, len(d), 2)]
 
 
 def _arrivals(plan, cores, topo, r):
-    tot = cn = 0
+    bn = cn = 0
     for s in plan[r]["rack"]:
-        for c, dests in plan[s]["sends"]:
-            if r in dests:
-                m = topo.mask(c, cores[r])
-                cn += len(_bits(m))
-                for grp in _groups(dests, m):
-                    for q, mm in grp:
-                        if q == r:
-                            tot += len(_bits(mm))
-    return tot, cn
+        for proxy in (False, True):
+            c = plan[s]["proxy"] if proxy else cores[s]
+            m = len(_bits(topo.mask(c, cores[plan[s]["order"][0]])))
+            for call in _sends(plan, s, proxy):
+                if r in call:
+                    cn += m
+                    bn += m // len(call)
+    return bn, cn
 
 
 def _dst(topo, d, c):
@@ -136,92 +130,28 @@ def _dst(topo, d, c):
     return DstId(rid=rid, pnc=pid)
 
 
-def _multi(g, topo, core, dests, ap, mask, sem, loc):
-    g.remote_dma_fused([RemoteDMATransfer(dst_ids=[_dst(topo, d, core) for d in dests], dma_engine_mask=mask, remote_sem=sem,
-                                          srcs=[ap], dsts=[ap for d in dests])], local_sem=loc)
-    return len(_bits(mask))
-
-
-def _send_bins(g, T, topo, core, plan, src, dests, twins):
-    mask = topo.mask(core, T.cores[dests[0]])
-    i = plan[src]["i"]
-    first = plan[src]["rack"][0] < plan[src]["other"][0]
-    fo = 0 if first else 960
-    done = 0
-    for grp in _groups(dests, mask):
-        trs = []
-        for q, m in grp:
-            e = plan[q]["twin"] if twins else q
-            s = T.bins[:, BIN0 + BW * e:BIN0 + BW * e + BW]
-            d = T.pw[:, BW * i:BW * i + BW] if twins else T.fw[:, fo + BW * i:fo + BW * i + BW]
-            trs.append(RemoteDMATransfer(dst_ids=[_dst(topo, T.cores[q], core)], dma_engine_mask=m,
-                                         remote_sem=T.sem.twd if twins else T.sem.own, srcs=[s], dsts=[d]))
-            done += len(_bits(m))
-        g.remote_dma_fused(trs, local_sem=T.sem.loc)
-    return done
-
-
-def _fill_ranges(plan, dests, own):
-    b = sorted(set(dests + [plan[q]["twin"] for q in dests] + own))
-    runs = []
-    for k in b:
-        if runs and runs[-1][1] == k and k - runs[-1][0] < 2:
-            runs[-1][1] = k + 1
-        else:
-            runs.append([k, k + 1])
-    return [(BIN0 + BW * a, BIN0 + BW * z) for a, z in runs]
-
-
 def rank_program(g, core, T, topo):
     plan = _plan(T.cores, topo)
-    rank = T.rank_of(core)
-    if rank is not None:
-        _rank(g, core, rank, T, topo, plan)
-        return
     for r in range(len(plan)):
-        for c, dests in plan[r]["sends"]:
-            if c == core:
-                _helper(g, core, r, dests, T, topo, plan)
+        if core == T.cores[r]:
+            _core(g, core, T, topo, plan, r, r)
+        elif core == plan[r]["proxy"]:
+            _core(g, core, T, topo, plan, r, plan[r]["twin"])
 
 
-def _helper(g, core, r, dests, T, topo, plan):
-    rc = T.cores[r]
-    onchip = topo.mask(rc, core)
-    offchip = topo.mask(core, T.cores[dests[0]])
-    i = plan[r]["i"]
-    nv = 0
-    for a, z in _fill_ranges(plan, dests, []):
-        g.vector.memset(T.bins[:, a:z], 0.0).then_inc(T.sem.sv, 1)
-        nv += 1
-    slot = T.craw[:, 64 + 8 * i:72 + 8 * i]
-    g.wait_ge(T.sem.cnt, len(_bits(topo.mask(rc, T.cores[plan[r]["sends"][0][1][0]]))))
-    loc = _multi(g, topo, core, [T.cores[q] for q in dests], slot, offchip, T.sem.cnt, T.sem.loc)
-    g.vector.wait_ge(T.sem.sv, nv)
-    g.vector.wait_ge(T.sem.sxr, len(_bits(onchip)))
-    g.vector.wait_ge(T.sem.offr, len(_bits(onchip & ~offchip)))
-    g.vector.tensor_copy(T.bins[:, 0:5120].indirect(T.off[:, 0:64]), T.xs[:, :]).then_inc(T.sem.sv, 1)
-    nv += 1
-    g.wait_ge(T.sem.sv, nv)
-    loc += _send_bins(g, T, topo, core, plan, r, dests, True)
-    loc += _send_bins(g, T, topo, core, plan, r, dests, False)
-    g.wait_ge(T.sem.loc, loc)
-
-
-def _rank(g, core, r, T, topo, plan):
+def _core(g, core, T, topo, plan, r, s):
     P = plan[r]
-    i, rack, twin = P["i"], P["rack"], P["twin"]
-    first = rack[0] < P["other"][0]
-    dests = P["sends"][0][1]
-    helpers = [c for c, d in P["sends"][1:]]
-    onchip = topo.mask(core, helpers[0])
-    offchip = topo.mask(core, T.cores[dests[0]])
-    inner = onchip & ~offchip
-    tot, cn = _arrivals(plan, T.cores, topo, r)
+    rack = P["rack"]
+    own = s == r
+    ebase = EL * rack[0]
+    offchip = topo.mask(core, T.cores[P["order"][0]])
+    nb = len(_bits(offchip))
 
     Q = {"v": g.vector, "t": g.tensor, "s": g.scalar, "g": g, "y": g.sync}
     S = {"v": T.sem.sv, "t": T.sem.st, "s": T.sem.ss, "g": T.sem.sg}
     n = {"v": 0, "t": 0, "s": 0, "g": 0}
     seen = {}
+    loc = [0]
 
     def did(q, ins):
         ins.then_inc(S[q], 1)
@@ -254,236 +184,185 @@ def _rank(g, core, r, T, topo, plan):
     def mm(out, l, rh, start, stop):
         return did("t", g.tensor.matmul(out, l, rh, start, stop))
 
-    for a in range(8):
-        q = g.sync if a % 2 == 0 else g.scalar
-        q.dma_start(T.exr[16 * a:16 * a + 16, :], T.ex[:, :]).then_inc(T.sem.sex, 16)
-    g.sync.dma_start(T.xs[:, :], T.x[:, :]).then_inc(T.sem.sx, 16)
+    def iota(out, pattern, base=0, mult=0):
+        return did("g", g.iota(out, pattern, base, mult, allow_small_or_imprecise_dtypes=True))
 
-    pi, gi, qi = T.icol[:, 0:1], T.icol[:, 1:2], T.icol[:, 2:3]
-    pf, gcol, qcol, q8 = T.fcol[:, 0:1], T.fcol[:, 1:2], T.fcol[:, 2:3], T.fcol[:, 3:4]
-    did("g", g.iota(T.am[:, :], [[1, 128]], 0, 0))
-    did("g", g.iota(T.v8[:, :], [[128, 8]], 0, 1))
+    if own:
+        g.scalar.dma_start(T.exc[:, :], T.ex[:, :]).then_inc(T.sem.sex, 16)
+        g.sync.dma_start(T.xs[:, :], T.x[:, :]).then_inc(T.sem.sx, 16)
+        ex_in, x_in = (T.sem.sex, 16), (T.sem.sx, 16)
+    else:
+        k = len(_bits(topo.mask(T.cores[s], core)))
+        ex_in, x_in = (T.sem["hex"], k), (T.sem.hx, k)
+
+    pi = T.pi[:, 0:1]
+    af, qf, pf, cf, gf, rf = [T.fcol[:, k:k + 1] for k in range(6)]
     G_pi = did("g", g.iota(pi, [[0, 1]], 0, 1))
-    fl = {"allow_small_or_imprecise_dtypes": True}
-    G_c2 = did("g", g.iota(T.c2[:, :], [[2, 64]], 0, 0, **fl))
-    G_p16 = did("g", g.iota(T.p16[:, :], [[0, 4], [16, 15]], 0, 0, **fl))
-    did("g", g.iota(T.k0[:, :], [[64, 4], [16, 15]], 0, 0, **fl))
-    if first:
-        G_xt = did("g", g.iota(T.xt[:, :], [[176, 4], [0, 15]], 0, 0, **fl))
-        k1 = T.k0
-    else:
-        did("g", g.iota(T.k1[:, :], [[240, 4], [16, 15]], 0, 0, **fl))
-        G_xt = did("g", g.iota(T.xt[:, :], [[-176, 4], [0, 15]], 960, 0, **fl))
-        k1 = T.k1
-
-    z0 = fill(T.zz[:, :], 0.0)
-    V_ones = fill(T.ones[:, :], 1.0)
+    G_p = iota(T.prow[:, :], [[1, 128]])
+    G_a = iota(T.arow[:, :], [[0, 16], [1, 8]])
+    G_h = iota(T.hrow[:, :], [[16, 8]])
+    G_q = iota(T.qrow[:, :], [[0, 8], [1, 16]])
     t = fill(T.rst[:, :], 1.0)
-
-    mx = {}
-    need("g", V_ones)
-    G_mx = None
-    for half in sorted(set([r % 2, twin % 2])):
-        m = T.mx0 if half == 0 else T.mx1
-        g0 = 4 * half
-        if G_mx is not None:
-            need("g", G_mx)
-        a = did("g", g.affine_select(T.mxa[:, :], T.ones[:, 0:NC], [[-16, 4], [0, 15]], Op.is_ge, 0.0, -16 * g0, 1))
-        need("g", a)
-        G_mx = did("g", g.affine_select(m[:, :], T.mxa[:, :], [[16, 4], [0, 15]], Op.is_ge, 0.0, 16 * g0 + 15, -1))
-        mx[half] = m
-
+    V_one = fill(T.ones[:, :], 1.0)
     need("v", t)
-    fill(T.rst[:, 0::64], 0.0)
+    fill(T.rst[:, 0::8], 0.0)
     need("v", G_pi)
-    ts(gi, pi, 4, Op.arith_shift_right)
-    ts(qi, pi, 15, Op.bitwise_and)
+    ts(T.ai[:, 0:1], pi, 7, Op.bitwise_and)
+    V_i = ts(T.qi[:, 0:1], pi, 3, Op.arith_shift_right)
     cp(pf, pi)
-    ts(T.am4[:, :], T.am[:, :], 4, Op.arith_shift_right)
-    ts(T.am15[:, :], T.am[:, :], 15, Op.bitwise_and)
-    t = ts(T.eci[:, :], T.v8[:, :], 4, Op.arith_shift_right)
+    need("v", V_i)
+    cp(af, T.ai[:, 0:1])
+    V_f = cp(qf, T.qi[:, 0:1])
+    need("v", V_f, G_p, G_a, G_h)
+    ts(T.dn0[:, :], T.prow[:, :], pf, Op.is_le, -1.0, Op.mult)
+    ts(T.samea[:, :], T.arow[:, :], af, Op.is_equal)
+    ts(T.blt[:, :], T.arow[:, :], af, Op.is_gt)
+    V_c = ts(cf, af, 128.0, Op.mult, qf, Op.add)
+    need("v", V_c)
+    tt(T.dneg[:, :], T.dn0[:, :], T.samea[:, :], Op.mult)
+    V_con = ts(T.colid[:, :], T.hrow[:, :], cf, Op.add)
+
+    if own:
+        far = plan[P["twin"]]["proxy"]
+        rid, pid = topo.addr(far, core)
+        m = topo.mask(core, far)
+        g.wait_ge(*ex_in)
+        g.remote_dma(T.exc[:, :], T.exc[:, :], T.sem["hex"], T.sem.loc, pid, rid, m)
+        g.wait_ge(*x_in)
+        g.remote_dma(T.xs[:, :], T.xs[:, :], T.sem.hx, T.sem.loc, pid, rid, m)
+        loc[0] += 2 * len(_bits(m))
+        G_g = iota(T.grow[:, :], [[1, 4], [0, 16]])
+        G_kk = iota(T.kk[:, :], [[64, 4], [16, NM]])
+        G_nm = iota(T.nm[:, 0:NM], [[-16, NM]])
+
+    g.vector.wait_ge(*ex_in)
+    t = ts(T.exf[:, :], T.exc[:, :], float(ebase), Op.subtract)
     need("v", t)
-    cp(T.ecol[:, :], T.eci[:, :])
-    V_w = ts(T.wcol[:, :], T.eci[:, :], 64.0, Op.mult, float(BIN0), Op.add)
-    cp(gcol, gi)
-    V_q = cp(qcol, qi)
-    ts(q8, qi, 0.125, Op.mult)
-    t = ts(T.nba[:, :], T.am[:, :], pf, Op.is_le, -1.0, Op.mult)
-    need("v", V_q)
-    ts(T.sm[:, :], T.am15[:, :], qcol, Op.is_equal)
-    t = ts(T.sameg[:, :], T.am4[:, :], gcol, Op.is_equal)
+    for h in range(8):
+        V_oh = ts(T.oh[:, h::8], T.prow[:, 0:NE], T.exf[:, h:h + 1], Op.is_equal)
+    need("v", V_oh)
+    V_inc = did("v", g.vector.tensor_tensor_scan(T.inc[:, :], T.rst[:, :], T.oh[:, :], 0.0, Op.mult, Op.add))
+    need("t", V_con, V_oh)
+    mm(T.pl[:, 0:256], T.dneg[:, :], T.oh[:, :], True, False)
+    need("t", V_inc)
+    for h in range(8):
+        mm(T.pl[:, h:256:8], T.blt[:, :], T.inc[:, 7::8], False, False)
+    T_pl = mm(T.pl[:, 0:256], T.samea[:, :], T.inc[:, :], False, True)
+    need("v", V_inc)
+    V_cnt = cp(T.craw[:, NE * s:NE * s + NE], T.inc[:, 7::8])
+    ts(T.ex4[:, :], T.exc[:, :], float(ebase), Op.subtract, 4.0, Op.mult)
+    need("v", T_pl)
+    V_pr = tt(T.pr[:, :], T.pl[:, 0:256], T.oh[:, :], Op.mult)
+    need("v", V_pr)
+    need("s", V_pr)
+    for h in range(5, 8):
+        S_plc = act(T.junk[:, 32 * h:32 * h + 32], T.pr[:, h::8], accum_out=T.plc[:, h:h + 1])
+    for h in range(5):
+        V_plc = did("v", g.vector.tensor_reduce(T.plc[:, h:h + 1], T.pr[:, h::8], Ax.X, Op.add))
+    need("v", V_plc, S_plc)
+    t = cp(T.pli[:, :], T.plc[:, :])
     need("v", t)
-    tt(T.nb[:, :], T.nba[:, :], T.sameg[:, :], Op.mult)
-
-    need("s", z0)
-    for a, z in _fill_ranges(plan, dests, [r, twin]):
-        S_fill = act(T.bins[:, a:z], T.zz[:, 0:z - a])
-
-    g.vector.wait_ge(T.sem.sex, 128)
-    V_oh = []
-    for k in range(8):
-        V_oh.append(ts(T.oh[:, 64 * k:64 * k + 64], T.exr[:, :], T.ecol[:, k:k + 1], Op.is_equal))
-    V_scan = []
-    need("v", V_oh[7])
-    for h in range(2):
-        w = slice(256 * h, 256 * h + 256)
-        V_scan.append(did("v", g.vector.tensor_tensor_scan(T.inc[:, w], T.rst[:, w], T.oh[:, w], 0.0, Op.mult, Op.add)))
-    for k in range(8):
-        need("s", V_oh[k], V_w)
-        S_ohw = act(T.ohw[:, 64 * k:64 * k + 64], T.oh[:, 64 * k:64 * k + 64], scale=T.wcol[:, k:k + 1])
-    need("t", V_oh[7])
-    T_pl = []
-    mm(T.pl0[:, 0:256], T.nb[:, :], T.oh[:, 0:256], True, False)
-    mm(T.pl1[:, 0:256], T.nb[:, :], T.oh[:, 256:512], True, False)
-    for h in range(2):
-        need("t", V_scan[h])
-        T_pl.append(mm((T.pl0 if h == 0 else T.pl1)[:, 0:256], T.sameg[:, :], T.inc[:, 256 * h:256 * h + 256], False, True))
-    need("v", V_scan[1])
-    V_cnt = cp(T.craw[:, 64 + 8 * i:72 + 8 * i], T.inc[:, 63::64])
-    n0, n1, n2 = T.nt[:, 0:64], T.nt[:, 64:128], T.nt[:, 128:192]
-    ts(n1, T.exr[:, :], 0.0, Op.is_lt, q8, Op.mult)
-    t = ts(n0, T.exr[:, :], 0.0, Op.is_lt)
-    need("v", t, G_c2)
-    V_n = tt(n2, n0, T.c2[:, :], Op.mult)
-    V_pr = []
-    for h in range(2):
-        need("v", T_pl[h])
-        w = slice(256 * h, 256 * h + 256)
-        V_pr.append(tt(T.pr[:, w], (T.pl0 if h == 0 else T.pl1)[:, 0:256], T.oh[:, w], Op.mult))
-    sl = T.pslot[:, 0:64]
-    need("t", S_ohw)
-    for k in range(8):
-        mm(sl, T.sm[:, :], T.ohw[:, 64 * k:64 * k + 64], k == 0, False)
-    need("t", V_n)
-    mm(sl, T.sm[:, :], n1, False, False)
-    mm(sl, T.sm[:, :], n2, False, False)
-    for k in range(8):
-        need("t", V_pr[k // 4])
-        T_sl = mm(sl, T.sm[:, :], T.pr[:, 64 * k:64 * k + 64], False, k == 7)
-    need("v", T_sl)
-    V_off = cp(T.off[:, :], sl)
-    need("v", V_off, S_fill)
-    g.vector.wait_ge(T.sem.sx, 16)
-    V_sc = cp(T.bins[:, 0:5120].indirect(T.off[:, 0:64]), T.xs[:, :])
-
-    g.wait_ge(T.sem.sx, 16)
-    loc = _multi(g, topo, core, helpers, T.xs[:, :], onchip, T.sem.sxr, T.sem.loc)
-    need("g", V_cnt)
-    loc += _multi(g, topo, core, helpers + [T.cores[q] for q in dests], T.craw[:, 64 + 8 * i:72 + 8 * i], offchip,
-                  T.sem.cnt, T.sem.loc)
-    need("g", V_off)
-    loc += _multi(g, topo, core, helpers, T.off[:, :], inner, T.sem.offr, T.sem.loc)
-    need("g", V_sc)
-    loc += _send_bins(g, T, topo, core, plan, r, dests, True)
-    loc += _send_bins(g, T, topo, core, plan, r, dests, False)
-    if first:
-        g.wait_ge(T.sem.cnt, cn)
-        rid, pid = topo.addr(T.cores[twin], core)
-        g.remote_dma(T.craw[:, 0:64], T.craw[:, 64:128], T.sem.cntf, T.sem.loc, pid, rid, offchip)
-        loc += len(_bits(offchip))
-
-    fo, ptw = (0, 2048) if first else (960, 0)
-    need("s", V_sc)
-    act(T.pw[:, BW * i:BW * i + BW], T.bins[:, BIN0 + BW * twin:BIN0 + BW * twin + BW])
-    S_own = act(T.fw[:, fo + BW * i:fo + BW * i + BW], T.bins[:, BIN0 + BW * r:BIN0 + BW * r + BW])
-
-    ts(T.idm[:, :], T.am[:, :], pf, Op.is_equal)
-    ts(T.id256[:, :], T.am[:, :], pf, Op.is_equal, 256.0, Op.mult)
-    fill(T.nones[:, :], -1.0)
-    fill(T.c248[:, :], 248.0)
-    fill(T.rb0[:, 0:NC], 0.0)
-    if first:
-        fill(T.rb1[:, 0:NC], 0.0)
-    else:
-        ts(T.nid[:, :], T.am[:, :], pf, Op.is_equal, -1.0, Op.mult)
-        fill(T.fw[:, 960 + 2048:FWW], 0.0)
-    fill(T.pw[:, PWZ:PWW], 0.0)
-    need("v", G_mx, G_p16)
-    t = ts(T.pc[:, :], T.p16[:, :], qcol, Op.add)
+    ts(T.mi[:, :], T.pli[:, :], 4, Op.arith_shift_right)
+    t = ts(T.ki[:, :], T.pli[:, :], 15, Op.bitwise_and)
     need("v", t)
-
-    def listing(u, owner, kk, before):
-        col = owner // 2
-        m = mx[owner % 2]
-        rb, po, out = (T.rb0, T.po0, T.offp) if u == 0 else (T.rb1, T.po1, T.offf)
-        ind, ic = T.ind[:, 8 * NC * u:8 * NC * u + 8 * NC], T.ic[:, 8 * NC * u:8 * NC * u + 8 * NC]
-        io, w = 8 * NC * u, 8 * NC
-        lo, ns = (0, 16) if before else (64, 8)
-        cb = 0 if u == 0 else 8
-        t = did("v", g.vector.tensor_tensor_scan(T.cum[:, cb:cb + ns], T.craw[:, lo + col::8], T.c248[:, 0:ns], 0.0,
-                                                 Op.add, Op.min))
-        need("v", t)
-        if before:
-            ts(rb[:, 0:NC], m[:, :], T.cum[:, cb + 7:cb + 8], Op.mult)
-            cb += 8
-        for s in range(8):
-            t = ts(rb[:, NC * (s + 1):NC * (s + 2)], m[:, :], T.cum[:, cb + s:cb + s + 1], Op.mult)
+    tt(T.wf[:, :], T.ex4[:, :], T.mi[:, :], Op.add)
+    t = cp(T.kf[:, :], T.ki[:, :])
+    need("v", t, G_q)
+    for h in range(8):
+        w = slice(128 * h, 128 * h + 128)
+        ts(T.lh[:, w], T.qrow[:, :], T.kf[:, h:h + 1], Op.is_equal)
+        t = ts(T.rh[:, w], T.prow[:, :], T.wf[:, h:h + 1], Op.is_equal, T.colid[:, h:h + 1], Op.mult)
         need("t", t)
-        if before:
-            mm(T.pbt[:, 0:NC], T.ones[:, :], rb[:, 0:NC], True, True)
-        t_b = mm(T.pb[:, 0:w], T.ones[:, :], rb[:, NC:9 * NC], True, True)
-        mm(T.pcn[:, 0:w], T.nones[:, :], rb[:, NC:9 * NC], True, False)
-        t_c = mm(T.pcn[:, 0:w], T.ones[:, :], rb[:, 0:w], False, True)
-        need("v", t_b)
-        if before:
-            tt(T.indt[:, :], T.pc[:, :], T.pbt[:, 0:NC], Op.is_ge)
-        for s in range(8):
-            v_i = tt(T.ind[:, io + NC * s:io + NC * s + NC], T.pc[:, :], T.pb[:, NC * s:NC * s + NC], Op.is_ge)
-        need("v", t_c, v_i)
-        v_c = tt(ic, ind, T.pcn[:, 0:w], Op.mult)
-        extra = []
-        if u == 1:
-            need("v", G_xt)
-            v_c = tt(T.ix[:, :], T.indt[:, :] if before else T.ind[:, io + NC * 7:io + NC * 8], T.xt[:, :], Op.mult)
-            extra.append((T.idm, T.ix))
-            if before:
-                v_c = tt(T.ib[:, :], T.indt[:, :], T.pbt[:, 0:NC], Op.mult)
-                extra.append((T.nid, T.ib))
-        o = po[:, 0:NC]
-        need("t", G_xt, v_i)
-        mm(o, T.idm[:, :], kk[:, :], True, False)
-        for s in range(8):
-            mm(o, T.id256[:, :], T.ind[:, io + NC * s:io + NC * s + NC], False, False)
-        need("t", v_c)
-        for l, rh in extra:
-            mm(o, l[:, :], rh[:, :], False, False)
-        for s in range(8):
-            t = mm(o, T.idm[:, :], T.ic[:, io + NC * s:io + NC * s + NC], False, s == 7)
-        need("v", t)
-        return ts(out[:, :], o, qcol, Op.add)
+        T_li = mm(T.plist[:, 0:128], T.lh[:, w], T.rh[:, w], h == 0, h == 7)
+    need("v", T_li)
+    V_off = cp(T.off[:, :], T.plist[:, 0:128])
 
+    need("g", V_cnt)
+    cdst = P["order"] + ([] if own else [r])
+    slot = T.craw[:, NE * s:NE * s + NE]
+    g.remote_dma_fused([RemoteDMATransfer(dst_ids=[_dst(topo, T.cores[q], core) for q in cdst], dma_engine_mask=offchip,
+                                          remote_sem=T.sem.cnt, srcs=[slot], dsts=[slot for q in cdst])], local_sem=T.sem.loc)
+    loc[0] += nb
+    need("v", V_off)
+    need("s", V_off)
+    g.vector.wait_ge(*x_in)
+    g.scalar.wait_ge(*x_in)
+    land = T.fw[:, BW * s:BW * s + BW]
+    for call in _sends(plan, r, not own):
+        masks = _halves(offchip) if len(call) == 2 else (offchip,)
+        trs = []
+        for k, q in enumerate(call):
+            d = rack.index(q)
+            b = T.bins[:, BW * d:BW * d + BW]
+            src = T.xs[:, :].indirect(T.off[:, 16 * d:16 * d + 16])
+            need("g", cp(b, src) if k == 0 else act(b, src))
+            trs.append(RemoteDMATransfer(dst_ids=[_dst(topo, T.cores[q], core)], dma_engine_mask=masks[k],
+                                         remote_sem=T.sem["bin"], srcs=[b], dsts=[land]))
+        g.remote_dma_fused(trs, local_sem=T.sem.loc)
+        loc[0] += nb
+
+    if own:
+        d = rack.index(r)
+        act(land, T.xs[:, :].indirect(T.off[:, 16 * d:16 * d + 16]))
+        _merge(g, core, T, topo, plan, r, dict(need=need, did=did, ts=ts, tt=tt, cp=cp, fill=fill, act=act, mm=mm, n=n,
+                                               V_one=V_one, G_g=G_g, G_kk=G_kk, G_nm=G_nm, cols=(pi, pf, gf, rf)))
+    g.wait_ge(T.sem.loc, loc[0])
+    for q in ("v", "t", "s", "g"):
+        need("g", (q, n[q]))
+    if own:
+        g.wait_ge(T.sem.sy, 32)
+
+
+def _merge(g, core, T, topo, plan, r, c):
+    need, did, ts, tt, cp, fill, act, mm, n = [c[k] for k in ("need", "did", "ts", "tt", "cp", "fill", "act", "mm", "n")]
+    pi, pf, gf, rf = c["cols"]
+    bn, cn = _arrivals(plan, T.cores, topo, r)
+    fill(T.fw[:, ZC:FWW], 0.0)
+    ts(T.gi[:, 0:1], pi, 4, Op.arith_shift_right)
+    t = ts(T.ri[:, 0:1], pi, 15, Op.bitwise_and)
+    ts(T.idm[:, :], T.prow[:, :], pf, Op.is_equal)
+    need("v", t)
+    cp(gf, T.gi[:, 0:1])
+    t = cp(rf, T.ri[:, 0:1])
+    need("v", t, c["G_g"], c["G_kk"], c["G_nm"])
+    ts(T.tri0[:, :], T.prow[:, 0:64], pf, Op.is_ge)
+    t = ts(T.tri1[:, :], T.grow[:, :], gf, Op.is_equal)
+    ts(T.sel[:, 0:EL], T.prow[:, 0:EL], gf, Op.is_equal)
+    ts(T.kq[:, :], T.kk[:, :], 0.0, Op.mult, rf, Op.add)
+    need("v", t)
+    V_con = tt(T.tri[:, :], T.tri0[:, :], T.tri1[:, :], Op.mult)
+    need("t", V_con, c["V_one"])
+    mm(T.po[:, 0:60], T.idm[:, :], T.kk[:, :], True, False)
+
+    d = plan[r]["rack"].index(r)
     g.vector.wait_ge(T.sem.cnt, cn)
-    V_lp = listing(0, twin, T.k0, False)
-    need("v", V_lp, S_own)
-    need("s", V_lp, S_own)
-    g.vector.wait_ge(T.sem.twd, tot)
-    V_pk = cp(T.pk[:, 0:480], T.pw[:, :].indirect(T.offp[:, 0:30]))
-    g.scalar.wait_ge(T.sem.twd, tot)
-    S_pk = act(T.pk[:, 480:960], T.pw[:, :].indirect(T.offp[:, 30:60]))
-    need("g", V_pk, S_pk)
-    tp = 0 if first else 2048
-    rid, pid = topo.addr(T.cores[twin], core)
-    g.remote_dma(T.fw[:, tp:tp + 960], T.pk[:, :], T.sem.pkd, T.sem.loc, pid, rid, offchip)
-    loc += len(_bits(offchip))
-
-    npk = len(_bits(topo.mask(T.cores[twin], core)))
-    if not first:
-        g.vector.wait_ge(T.sem.cntf, npk)
-    V_lf = listing(1, r, k1, not first)
-    need("v", V_lf)
-    need("s", V_lf)
-    fe = 3008 if first else FWW
+    for e in range(EL):
+        t = cp(T.cc[:, 16 * e:16 * e + 16], T.craw[:, EL * d + e::NE])
+    need("t", t)
+    t = mm(T.pc[0:64, 0:1], T.cc[:, :], T.ones[:, 0:1], True, True)
+    need("v", t)
+    t = cp(T.cb[0:64, 0:1], T.pc[0:64, 0:1])
+    ts(T.nc[0:64, 0:1], T.pc[0:64, 0:1], -1.0, Op.mult, 256.0, Op.add)
+    need("t", t)
+    t = mm(T.pb[0:64, 0:1], T.tri[0:64, :], T.cb[0:64, 0:1], True, True)
+    need("v", t)
+    t = ts(T.bm[0:64, 0:NM], T.nm[0:64, 0:NM], T.pb[0:64, 0:1], Op.add)
+    need("v", t)
+    for m in range(NM):
+        w = T.ind[0:64, 128 * m:128 * m + 128]
+        t = ts(w, T.qrow[0:64, :], T.bm[0:64, m:m + 1], Op.is_ge, T.nc[0:64, 0:1], Op.mult)
+        need("t", t)
+        mm(T.po[:, m:60:NM], w, T.sel[0:64, 0:EL], False, False)
+    t = mm(T.po[:, 0:60], T.idm[:, :], T.kq[:, :], False, True)
+    need("v", t)
+    V_l = cp(T.offf[:, :], T.po[:, 0:60])
+    need("v", V_l, ("s", n["s"]))
+    need("s", V_l, ("s", n["s"]))
     for q in (g.vector, g.scalar):
-        q.wait_ge(T.sem.own, tot)
-        q.wait_ge(T.sem.pkd, npk)
-    V_y = cp(T.yt[:, 0:480], T.fw[:, 0:fe].indirect(T.offf[:, 0:30]))
-    S_y = act(T.yt[:, 480:960], T.fw[:, 0:fe].indirect(T.offf[:, 30:60]))
+        q.wait_ge(T.sem["bin"], bn)
+    V_y = cp(T.yt[:, 0:480], T.fw[:, :].indirect(T.offf[:, 0:30]))
+    S_y = act(T.yt[:, 480:960], T.fw[:, :].indirect(T.offf[:, 30:60]))
     need("y", V_y)
     g.sync.dma_start(T.y[:, 0:480], T.yt[:, 0:480]).then_inc(T.sem.sy, 16)
     need("s", S_y)
     g.scalar.dma_start(T.y[:, 480:960], T.yt[:, 480:960]).then_inc(T.sem.sy, 16)
-
-    g.wait_ge(T.sem.loc, loc)
-    for q in ("v", "t", "s", "g"):
-        need("g", (q, n[q]))
-    g.wait_ge(T.sem.sy, 32)

@@ -7,6 +7,7 @@ NE = 32
 ZC = 4096
 FWW = ZC + 432
 NM = 15
+XH = 768
 
 SCRATCH = {
     "xs": ("sbuf", [128, 1024], "bfloat16"),
@@ -68,7 +69,7 @@ SCRATCH = {
     "pb": ("psum", [128, 512], "float32"),
     "po": ("psum", [128, 512], "float32"),
 }
-SEMAPHORES = ["sv", "st", "ss", "sg", "sex", "sx", "hex", "hx", "loc", "cnt", "bin", "sy"]
+SEMAPHORES = ["sv", "st", "ss", "sg", "sex", "sx", "sxh", "hex", "hx", "loc", "cnt", "bin", "sy"]
 
 _memo = {}
 
@@ -100,9 +101,11 @@ def _plan(cores, topo):
         for k in range(max(len(same), len(cross))):
             order += cross[k:k + 1] + same[k:k + 1]
         base = c - c % topo.CORES_PER_CHIP
-        proxy = [h for h in range(base, base + topo.CORES_PER_CHIP)
-                 if topo.die(h) != topo.die(c) and all(topo.may_write(h, cores[q]) for q in peers)][0]
-        plan.append({"rack": rack, "twin": twin, "order": order, "proxy": proxy})
+        chip = range(base, base + topo.CORES_PER_CHIP)
+        port = [h for h in chip if all(topo.may_write(h, cores[q]) for q in peers)]
+        proxy = [h for h in port if topo.die(h) != topo.die(c)][0]
+        helper = [h for h in chip if topo.die(h) == topo.die(c) and h not in port][0]
+        plan.append({"rack": rack, "twin": twin, "order": order, "proxy": proxy, "helper": helper})
     _memo["plan"] = plan
     return plan
 
@@ -130,6 +133,13 @@ def _dst(topo, d, c):
     return DstId(rid=rid, pnc=pid)
 
 
+def _cables(plan, cores, topo, r):
+    far = plan[plan[r]["twin"]]["proxy"]
+    m = topo.mask(cores[r], far)
+    hop = _halves(m & topo.mask(cores[r], plan[r]["helper"]))[1]
+    return far, m, hop, _halves(topo.mask(plan[r]["helper"], far))[0]
+
+
 def rank_program(g, core, T, topo):
     plan = _plan(T.cores, topo)
     for r in range(len(plan)):
@@ -137,6 +147,12 @@ def rank_program(g, core, T, topo):
             _core(g, core, T, topo, plan, r, r)
         elif core == plan[r]["proxy"]:
             _core(g, core, T, topo, plan, r, plan[r]["twin"])
+        elif core == plan[r]["helper"]:
+            far, m, hop, mh = _cables(plan, T.cores, topo, r)
+            rid, pid = topo.addr(far, core)
+            g.wait_ge(T.sem.hx, len(_bits(hop)))
+            g.remote_dma(T.xs[:, XH:1024], T.xs[:, XH:1024], T.sem.hx, T.sem.loc, pid, rid, mh)
+            g.wait_ge(T.sem.loc, len(_bits(mh)))
 
 
 def _core(g, core, T, topo, plan, r, s):
@@ -187,13 +203,14 @@ def _core(g, core, T, topo, plan, r, s):
     def iota(out, pattern, base=0, mult=0):
         return did("g", g.iota(out, pattern, base, mult, allow_small_or_imprecise_dtypes=True))
 
+    far, m, hop, mh = _cables(plan, T.cores, topo, s)
     if own:
         g.scalar.dma_start(T.exc[:, :], T.ex[:, :]).then_inc(T.sem.sex, 16)
-        g.sync.dma_start(T.xs[:, :], T.x[:, :]).then_inc(T.sem.sx, 16)
-        ex_in, x_in = (T.sem.sex, 16), (T.sem.sx, 16)
+        g.sync.dma_start(T.xs[:, XH:1024], T.x[:, XH:1024]).then_inc(T.sem.sxh, 16)
+        g.sync.dma_start(T.xs[:, 0:XH], T.x[:, 0:XH]).then_inc(T.sem.sx, 16)
+        ex_in, x_in = (T.sem.sex, 16), [(T.sem.sxh, 16), (T.sem.sx, 16)]
     else:
-        k = len(_bits(topo.mask(T.cores[s], core)))
-        ex_in, x_in = (T.sem["hex"], k), (T.sem.hx, k)
+        ex_in, x_in = (T.sem["hex"], len(_bits(m))), [(T.sem.hx, len(_bits(m)) + len(_bits(mh)))]
 
     pi = T.pi[:, 0:1]
     af, qf, pf, cf, gf, rf = [T.fcol[:, k:k + 1] for k in range(6)]
@@ -201,7 +218,6 @@ def _core(g, core, T, topo, plan, r, s):
     G_p = iota(T.prow[:, :], [[1, 128]])
     G_a = iota(T.arow[:, :], [[0, 16], [1, 8]])
     G_h = iota(T.hrow[:, :], [[16, 8]])
-    G_q = iota(T.qrow[:, :], [[0, 8], [1, 16]])
     t = fill(T.rst[:, :], 1.0)
     V_one = fill(T.ones[:, :], 1.0)
     need("v", t)
@@ -223,14 +239,17 @@ def _core(g, core, T, topo, plan, r, s):
     V_con = ts(T.colid[:, :], T.hrow[:, :], cf, Op.add)
 
     if own:
-        far = plan[P["twin"]]["proxy"]
         rid, pid = topo.addr(far, core)
-        m = topo.mask(core, far)
+        hrid, hpid = topo.addr(P["helper"], core)
         g.wait_ge(*ex_in)
         g.remote_dma(T.exc[:, :], T.exc[:, :], T.sem["hex"], T.sem.loc, pid, rid, m)
-        g.wait_ge(*x_in)
-        g.remote_dma(T.xs[:, :], T.xs[:, :], T.sem.hx, T.sem.loc, pid, rid, m)
-        loc[0] += 2 * len(_bits(m))
+        g.wait_ge(*x_in[0])
+        g.remote_dma(T.xs[:, XH:1024], T.xs[:, XH:1024], T.sem.hx, T.sem.loc, hpid, hrid, hop)
+        g.wait_ge(*x_in[1])
+        g.remote_dma(T.xs[:, 0:XH], T.xs[:, 0:XH], T.sem.hx, T.sem.loc, pid, rid, m)
+        loc[0] += 2 * len(_bits(m)) + len(_bits(hop))
+    G_q = iota(T.qrow[:, :], [[0, 8], [1, 16]])
+    if own:
         G_g = iota(T.grow[:, :], [[1, 4], [0, 16]])
         G_kk = iota(T.kk[:, :], [[64, 4], [16, NM]])
         G_nm = iota(T.nm[:, 0:NM], [[-16, NM]])
@@ -285,8 +304,9 @@ def _core(g, core, T, topo, plan, r, s):
     loc[0] += nb
     need("v", V_off)
     need("s", V_off)
-    g.vector.wait_ge(*x_in)
-    g.scalar.wait_ge(*x_in)
+    for w in x_in:
+        g.vector.wait_ge(*w)
+        g.scalar.wait_ge(*w)
     land = T.fw[:, BW * s:BW * s + BW]
     for call in _sends(plan, r, not own):
         masks = _halves(offchip) if len(call) == 2 else (offchip,)

@@ -7,7 +7,8 @@ NE = 32
 ZC = 4096
 FWW = ZC + 432
 NM = 15
-XH = 768
+XH = 512
+XW = 256
 
 SCRATCH = {
     "xs": ("sbuf", [128, 1024], "bfloat16"),
@@ -104,8 +105,9 @@ def _plan(cores, topo):
         chip = range(base, base + topo.CORES_PER_CHIP)
         port = [h for h in chip if all(topo.may_write(h, cores[q]) for q in peers)]
         proxy = [h for h in port if topo.die(h) != topo.die(c)][0]
-        helper = [h for h in chip if topo.die(h) == topo.die(c) and h not in port][0]
-        plan.append({"rack": rack, "twin": twin, "order": order, "proxy": proxy, "helper": helper})
+        rest = [h for h in chip if h not in port]
+        helpers = [[h for h in rest if (topo.die(h) == topo.die(c)) == near][0] for near in (True, False)]
+        plan.append({"rack": rack, "twin": twin, "order": order, "proxy": proxy, "helpers": helpers})
     _memo["plan"] = plan
     return plan
 
@@ -136,8 +138,11 @@ def _dst(topo, d, c):
 def _cables(plan, cores, topo, r):
     far = plan[plan[r]["twin"]]["proxy"]
     m = topo.mask(cores[r], far)
-    hop = _halves(m & topo.mask(cores[r], plan[r]["helper"]))[1]
-    return far, m, hop, _halves(topo.mask(plan[r]["helper"], far))[0]
+    return far, m, _halves(m), [_halves(topo.mask(h, far))[0] for h in plan[r]["helpers"]]
+
+
+def _part(T, k):
+    return T.xs[:, XH + XW * k:XH + XW * k + XW]
 
 
 def rank_program(g, core, T, topo):
@@ -147,12 +152,13 @@ def rank_program(g, core, T, topo):
             _core(g, core, T, topo, plan, r, r)
         elif core == plan[r]["proxy"]:
             _core(g, core, T, topo, plan, r, plan[r]["twin"])
-        elif core == plan[r]["helper"]:
+        elif core in plan[r]["helpers"]:
+            k = plan[r]["helpers"].index(core)
             far, m, hop, mh = _cables(plan, T.cores, topo, r)
             rid, pid = topo.addr(far, core)
-            g.wait_ge(T.sem.hx, len(_bits(hop)))
-            g.remote_dma(T.xs[:, XH:1024], T.xs[:, XH:1024], T.sem.hx, T.sem.loc, pid, rid, mh)
-            g.wait_ge(T.sem.loc, len(_bits(mh)))
+            g.wait_ge(T.sem.hx, len(_bits(hop[k])))
+            g.remote_dma(_part(T, k), _part(T, k), T.sem.hx, T.sem.loc, pid, rid, mh[k])
+            g.wait_ge(T.sem.loc, len(_bits(mh[k])))
 
 
 def _core(g, core, T, topo, plan, r, s):
@@ -210,7 +216,7 @@ def _core(g, core, T, topo, plan, r, s):
         g.sync.dma_start(T.xs[:, 0:XH], T.x[:, 0:XH]).then_inc(T.sem.sx, 16)
         ex_in, x_in = (T.sem.sex, 16), [(T.sem.sxh, 16), (T.sem.sx, 16)]
     else:
-        ex_in, x_in = (T.sem["hex"], len(_bits(m))), [(T.sem.hx, len(_bits(m)) + len(_bits(mh)))]
+        ex_in, x_in = (T.sem["hex"], len(_bits(m))), [(T.sem.hx, sum(len(_bits(w)) for w in [m] + mh))]
 
     pi = T.pi[:, 0:1]
     af, qf, pf, cf, gf, rf = [T.fcol[:, k:k + 1] for k in range(6)]
@@ -240,14 +246,15 @@ def _core(g, core, T, topo, plan, r, s):
 
     if own:
         rid, pid = topo.addr(far, core)
-        hrid, hpid = topo.addr(P["helper"], core)
         g.wait_ge(*ex_in)
         g.remote_dma(T.exc[:, :], T.exc[:, :], T.sem["hex"], T.sem.loc, pid, rid, m)
         g.wait_ge(*x_in[0])
-        g.remote_dma(T.xs[:, XH:1024], T.xs[:, XH:1024], T.sem.hx, T.sem.loc, hpid, hrid, hop)
+        g.remote_dma_fused([RemoteDMATransfer(dst_ids=[_dst(topo, h, core)], dma_engine_mask=hop[k], remote_sem=T.sem.hx,
+                                              srcs=[_part(T, k)], dsts=[_part(T, k)])
+                            for k, h in enumerate(P["helpers"])], local_sem=T.sem.loc)
         g.wait_ge(*x_in[1])
         g.remote_dma(T.xs[:, 0:XH], T.xs[:, 0:XH], T.sem.hx, T.sem.loc, pid, rid, m)
-        loc[0] += 2 * len(_bits(m)) + len(_bits(hop))
+        loc[0] += 3 * len(_bits(m))
     G_q = iota(T.qrow[:, :], [[0, 8], [1, 16]])
     if own:
         G_g = iota(T.grow[:, :], [[1, 4], [0, 16]])

from concourse.bass import DstId, RemoteDMATransfer
from concourse.mybir import AluOpType as Op, ActivationFunctionType as Act, AxisListType as Ax

EL = 4
BW = 256
NE = 32
ZC = 4096
FWW = ZC + 432
NM = 15
XH = 512
XW = 256

SCRATCH = {
    "xs": ("sbuf", [128, 1024], "bfloat16"),
    "exc": ("sbuf", [128, 8], "int32"),
    "bins": ("sbuf", [128, 2048], "bfloat16"),
    "fw": ("sbuf", [128, FWW], "bfloat16"),
    "yt": ("sbuf", [128, 960], "bfloat16"),
    "craw": ("sbuf", [128, 16 * NE], "bfloat16"),
    "pi": ("sbuf", [128, 8], "int32"),
    "ai": ("sbuf", [128, 8], "int32"),
    "qi": ("sbuf", [128, 8], "int32"),
    "gi": ("sbuf", [128, 8], "int32"),
    "ri": ("sbuf", [128, 8], "int32"),
    "fcol": ("sbuf", [128, 8], "float32"),
    "prow": ("sbuf", [128, 128], "bfloat16"),
    "arow": ("sbuf", [128, 128], "bfloat16"),
    "qrow": ("sbuf", [128, 128], "bfloat16"),
    "grow": ("sbuf", [128, 64], "bfloat16"),
    "hrow": ("sbuf", [128, 8], "float32"),
    "colid": ("sbuf", [128, 8], "float32"),
    "rst": ("sbuf", [128, 256], "bfloat16"),
    "ones": ("sbuf", [128, 8], "bfloat16"),
    "samea": ("sbuf", [128, 128], "bfloat16"),
    "blt": ("sbuf", [128, 128], "bfloat16"),
    "dn0": ("sbuf", [128, 128], "bfloat16"),
    "dneg": ("sbuf", [128, 128], "bfloat16"),
    "idm": ("sbuf", [128, 128], "bfloat16"),
    "tri0": ("sbuf", [128, 64], "bfloat16"),
    "tri1": ("sbuf", [128, 64], "bfloat16"),
    "tri": ("sbuf", [128, 64], "bfloat16"),
    "sel": ("sbuf", [128, 8], "bfloat16"),
    "kk": ("sbuf", [128, 60], "bfloat16"),
    "kq": ("sbuf", [128, 60], "bfloat16"),
    "nm": ("sbuf", [128, 16], "float32"),
    "exf": ("sbuf", [128, 8], "float32"),
    "ex4": ("sbuf", [128, 8], "float32"),
    "oh": ("sbuf", [128, 256], "bfloat16"),
    "inc": ("sbuf", [128, 256], "bfloat16"),
    "pr": ("sbuf", [128, 256], "bfloat16"),
    "junk": ("sbuf", [128, 256], "bfloat16"),
    "plc": ("sbuf", [128, 8], "float32"),
    "pli": ("sbuf", [128, 8], "int32"),
    "mi": ("sbuf", [128, 8], "int32"),
    "ki": ("sbuf", [128, 8], "int32"),
    "kf": ("sbuf", [128, 8], "float32"),
    "wf": ("sbuf", [128, 8], "float32"),
    "lh": ("sbuf", [128, 1024], "float16"),
    "rh": ("sbuf", [128, 1024], "float16"),
    "off": ("sbuf", [128, 128], "uint16"),
    "cc": ("sbuf", [128, 64], "bfloat16"),
    "cb": ("sbuf", [128, 8], "bfloat16"),
    "nc": ("sbuf", [128, 8], "float32"),
    "bm": ("sbuf", [128, 16], "float32"),
    "ind": ("sbuf", [128, NM * 128], "bfloat16"),
    "offf": ("sbuf", [128, 60], "uint16"),
    "pl": ("psum", [128, 512], "float32"),
    "plist": ("psum", [128, 512], "float32"),
    "pc": ("psum", [128, 512], "float32"),
    "pb": ("psum", [128, 512], "float32"),
    "po": ("psum", [128, 512], "float32"),
}
SEMAPHORES = ["sv", "st", "ss", "sg", "sex", "sx", "sxh", "hex", "hx", "loc", "cnt", "bin", "sy"]

_memo = {}


def _bits(mask):
    return [b for b in range(16) if mask >> b & 1]


def _halves(mask):
    b = _bits(mask)
    h = len(b) // 2
    return sum(1 << k for k in b[:h]), sum(1 << k for k in b[h:])


def _plan(cores, topo):
    if "plan" in _memo:
        return _memo["plan"]
    n = len(cores)
    plan = []
    for r in range(n):
        c = cores[r]
        rack = [q for q in range(n) if topo.rack(topo.host(cores[q])) == topo.rack(topo.host(c))]
        twin = [q for q in range(n) if q not in rack and topo.chip(cores[q]) == topo.chip(c) and topo.may_write(c, cores[q])][0]
        i = rack.index(r)
        peers = [rack[(i + d) % len(rack)] for d in range(1, len(rack))]
        same = [q for q in peers if topo.same_plane(c, cores[q])]
        cross = [q for q in peers if q not in same]
        order = []
        for k in range(max(len(same), len(cross))):
            order += cross[k:k + 1] + same[k:k + 1]
        base = c - c % topo.CORES_PER_CHIP
        chip = range(base, base + topo.CORES_PER_CHIP)
        port = [h for h in chip if all(topo.may_write(h, cores[q]) for q in peers)]
        proxy = [h for h in port if topo.die(h) != topo.die(c)][0]
        rest = [h for h in chip if h not in port]
        helpers = [[h for h in rest if (topo.die(h) == topo.die(c)) == near][0] for near in (True, False)]
        plan.append({"rack": rack, "twin": twin, "order": order, "proxy": proxy, "helpers": helpers})
    _memo["plan"] = plan
    return plan


def _sends(plan, r, proxy):
    d = plan[r]["order"] + ([r] if proxy else [])
    return [d[k:k + 2] for k in range(0, len(d), 2)]


def _arrivals(plan, cores, topo, r):
    bn = cn = 0
    for s in plan[r]["rack"]:
        for proxy in (False, True):
            c = plan[s]["proxy"] if proxy else cores[s]
            m = len(_bits(topo.mask(c, cores[plan[s]["order"][0]])))
            for call in _sends(plan, s, proxy):
                if r in call:
                    cn += m
                    bn += m // len(call)
    return bn, cn


def _dst(topo, d, c):
    rid, pid = topo.addr(d, c)
    return DstId(rid=rid, pnc=pid)


def _cables(plan, cores, topo, r):
    far = plan[plan[r]["twin"]]["proxy"]
    m = topo.mask(cores[r], far)
    return far, m, _halves(m), [_halves(topo.mask(h, far))[0] for h in plan[r]["helpers"]]


def _part(T, k):
    return T.xs[:, XH + XW * k:XH + XW * k + XW]


def rank_program(g, core, T, topo):
    plan = _plan(T.cores, topo)
    for r in range(len(plan)):
        if core == T.cores[r]:
            _core(g, core, T, topo, plan, r, r)
        elif core == plan[r]["proxy"]:
            _core(g, core, T, topo, plan, r, plan[r]["twin"])
        elif core in plan[r]["helpers"]:
            k = plan[r]["helpers"].index(core)
            far, m, hop, mh = _cables(plan, T.cores, topo, r)
            rid, pid = topo.addr(far, core)
            g.wait_ge(T.sem.hx, len(_bits(hop[k])))
            g.remote_dma(_part(T, k), _part(T, k), T.sem.hx, T.sem.loc, pid, rid, mh[k])
            g.wait_ge(T.sem.loc, len(_bits(mh[k])))


def _core(g, core, T, topo, plan, r, s):
    P = plan[r]
    rack = P["rack"]
    own = s == r
    ebase = EL * rack[0]
    offchip = topo.mask(core, T.cores[P["order"][0]])
    nb = len(_bits(offchip))

    Q = {"v": g.vector, "t": g.tensor, "s": g.scalar, "g": g, "y": g.sync}
    S = {"v": T.sem.sv, "t": T.sem.st, "s": T.sem.ss, "g": T.sem.sg}
    n = {"v": 0, "t": 0, "s": 0, "g": 0}
    seen = {}
    loc = [0]

    def did(q, ins):
        ins.then_inc(S[q], 1)
        n[q] += 1
        return (q, n[q])

    def need(q, *toks):
        for src, k in toks:
            if seen.get((q, src), 0) < k:
                Q[q].wait_ge(S[src], k)
                seen[(q, src)] = k

    def ts(out, in0, s1, op, s2=None, op1=None):
        if op1 is None:
            return did("v", g.vector.tensor_scalar(out, in0, s1, None, op))
        return did("v", g.vector.tensor_scalar(out, in0, s1, s2, op, op1))

    def tt(out, a, b, op):
        return did("v", g.vector.tensor_tensor(out, a, b, op))

    def cp(out, a):
        return did("v", g.vector.tensor_copy(out, a))

    def fill(ap, v):
        return did("v", g.vector.memset(ap, v))

    def act(out, in_, **kw):
        return did("s", g.scalar.activation(out, in_, Act.Copy, **kw))

    def mm(out, l, rh, start, stop):
        return did("t", g.tensor.matmul(out, l, rh, start, stop))

    def iota(out, pattern, base=0, mult=0):
        return did("g", g.iota(out, pattern, base, mult, allow_small_or_imprecise_dtypes=True))

    far, m, hop, mh = _cables(plan, T.cores, topo, s)
    if own:
        g.scalar.dma_start(T.exc[:, :], T.ex[:, :]).then_inc(T.sem.sex, 16)
        g.sync.dma_start(T.xs[:, XH:1024], T.x[:, XH:1024]).then_inc(T.sem.sxh, 16)
        g.sync.dma_start(T.xs[:, 0:XH], T.x[:, 0:XH]).then_inc(T.sem.sx, 16)
        ex_in, x_in = (T.sem.sex, 16), [(T.sem.sxh, 16), (T.sem.sx, 16)]
    else:
        ex_in, x_in = (T.sem["hex"], len(_bits(m))), [(T.sem.hx, sum(len(_bits(w)) for w in [m] + mh))]

    pi = T.pi[:, 0:1]
    af, qf, pf, cf, gf, rf = [T.fcol[:, k:k + 1] for k in range(6)]
    G_pi = did("g", g.iota(pi, [[0, 1]], 0, 1))
    G_p = iota(T.prow[:, :], [[1, 128]])
    G_a = iota(T.arow[:, :], [[0, 16], [1, 8]])
    G_h = iota(T.hrow[:, :], [[16, 8]])
    t = fill(T.rst[:, :], 1.0)
    V_one = fill(T.ones[:, :], 1.0)
    need("v", t)
    fill(T.rst[:, 0::8], 0.0)
    need("v", G_pi)
    ts(T.ai[:, 0:1], pi, 7, Op.bitwise_and)
    V_i = ts(T.qi[:, 0:1], pi, 3, Op.arith_shift_right)
    cp(pf, pi)
    need("v", V_i)
    cp(af, T.ai[:, 0:1])
    V_f = cp(qf, T.qi[:, 0:1])
    need("v", V_f, G_p, G_a, G_h)
    ts(T.dn0[:, :], T.prow[:, :], pf, Op.is_le, -1.0, Op.mult)
    ts(T.samea[:, :], T.arow[:, :], af, Op.is_equal)
    ts(T.blt[:, :], T.arow[:, :], af, Op.is_gt)
    V_c = ts(cf, af, 128.0, Op.mult, qf, Op.add)
    need("v", V_c)
    tt(T.dneg[:, :], T.dn0[:, :], T.samea[:, :], Op.mult)
    V_con = ts(T.colid[:, :], T.hrow[:, :], cf, Op.add)

    if own:
        rid, pid = topo.addr(far, core)
        g.wait_ge(*ex_in)
        g.remote_dma(T.exc[:, :], T.exc[:, :], T.sem["hex"], T.sem.loc, pid, rid, m)
        g.wait_ge(*x_in[0])
        g.remote_dma_fused([RemoteDMATransfer(dst_ids=[_dst(topo, h, core)], dma_engine_mask=hop[k], remote_sem=T.sem.hx,
                                              srcs=[_part(T, k)], dsts=[_part(T, k)])
                            for k, h in enumerate(P["helpers"])], local_sem=T.sem.loc)
        g.wait_ge(*x_in[1])
        g.remote_dma(T.xs[:, 0:XH], T.xs[:, 0:XH], T.sem.hx, T.sem.loc, pid, rid, m)
        loc[0] += 3 * len(_bits(m))
    G_q = iota(T.qrow[:, :], [[0, 8], [1, 16]])
    if own:
        G_g = iota(T.grow[:, :], [[1, 4], [0, 16]])
        G_kk = iota(T.kk[:, :], [[64, 4], [16, NM]])
        G_nm = iota(T.nm[:, 0:NM], [[-16, NM]])

    g.vector.wait_ge(*ex_in)
    t = ts(T.exf[:, :], T.exc[:, :], float(ebase), Op.subtract)
    need("v", t)
    for h in range(8):
        V_oh = ts(T.oh[:, h::8], T.prow[:, 0:NE], T.exf[:, h:h + 1], Op.is_equal)
    need("v", V_oh)
    V_inc = did("v", g.vector.tensor_tensor_scan(T.inc[:, :], T.rst[:, :], T.oh[:, :], 0.0, Op.mult, Op.add))
    need("t", V_con, V_oh)
    mm(T.pl[:, 0:256], T.dneg[:, :], T.oh[:, :], True, False)
    need("t", V_inc)
    for h in range(8):
        mm(T.pl[:, h:256:8], T.blt[:, :], T.inc[:, 7::8], False, False)
    T_pl = mm(T.pl[:, 0:256], T.samea[:, :], T.inc[:, :], False, True)
    need("v", V_inc)
    V_cnt = cp(T.craw[:, NE * s:NE * s + NE], T.inc[:, 7::8])
    ts(T.ex4[:, :], T.exc[:, :], float(ebase), Op.subtract, 4.0, Op.mult)
    need("v", T_pl)
    V_pr = tt(T.pr[:, :], T.pl[:, 0:256], T.oh[:, :], Op.mult)
    need("v", V_pr)
    need("s", V_pr)
    for h in range(5, 8):
        S_plc = act(T.junk[:, 32 * h:32 * h + 32], T.pr[:, h::8], accum_out=T.plc[:, h:h + 1])
    for h in range(5):
        V_plc = did("v", g.vector.tensor_reduce(T.plc[:, h:h + 1], T.pr[:, h::8], Ax.X, Op.add))
    need("v", V_plc, S_plc)
    t = cp(T.pli[:, :], T.plc[:, :])
    need("v", t)
    ts(T.mi[:, :], T.pli[:, :], 4, Op.arith_shift_right)
    t = ts(T.ki[:, :], T.pli[:, :], 15, Op.bitwise_and)
    need("v", t)
    tt(T.wf[:, :], T.ex4[:, :], T.mi[:, :], Op.add)
    t = cp(T.kf[:, :], T.ki[:, :])
    need("v", t, G_q)
    for h in range(8):
        w = slice(128 * h, 128 * h + 128)
        ts(T.lh[:, w], T.qrow[:, :], T.kf[:, h:h + 1], Op.is_equal)
        t = ts(T.rh[:, w], T.prow[:, :], T.wf[:, h:h + 1], Op.is_equal, T.colid[:, h:h + 1], Op.mult)
        need("t", t)
        T_li = mm(T.plist[:, 0:128], T.lh[:, w], T.rh[:, w], h == 0, h == 7)
    need("v", T_li)
    V_off = cp(T.off[:, :], T.plist[:, 0:128])

    need("g", V_cnt)
    cdst = P["order"] + ([] if own else [r])
    slot = T.craw[:, NE * s:NE * s + NE]
    g.remote_dma_fused([RemoteDMATransfer(dst_ids=[_dst(topo, T.cores[q], core) for q in cdst], dma_engine_mask=offchip,
                                          remote_sem=T.sem.cnt, srcs=[slot], dsts=[slot for q in cdst])], local_sem=T.sem.loc)
    loc[0] += nb
    need("v", V_off)
    need("s", V_off)
    for w in x_in:
        g.vector.wait_ge(*w)
        g.scalar.wait_ge(*w)
    land = T.fw[:, BW * s:BW * s + BW]
    for call in _sends(plan, r, not own):
        masks = _halves(offchip) if len(call) == 2 else (offchip,)
        trs = []
        for k, q in enumerate(call):
            d = rack.index(q)
            b = T.bins[:, BW * d:BW * d + BW]
            src = T.xs[:, :].indirect(T.off[:, 16 * d:16 * d + 16])
            need("g", cp(b, src) if k == 0 else act(b, src))
            trs.append(RemoteDMATransfer(dst_ids=[_dst(topo, T.cores[q], core)], dma_engine_mask=masks[k],
                                         remote_sem=T.sem["bin"], srcs=[b], dsts=[land]))
        g.remote_dma_fused(trs, local_sem=T.sem.loc)
        loc[0] += nb

    if own:
        d = rack.index(r)
        act(land, T.xs[:, :].indirect(T.off[:, 16 * d:16 * d + 16]))
        _merge(g, core, T, topo, plan, r, dict(need=need, did=did, ts=ts, tt=tt, cp=cp, fill=fill, act=act, mm=mm, n=n,
                                               V_one=V_one, G_g=G_g, G_kk=G_kk, G_nm=G_nm, cols=(pi, pf, gf, rf)))
    g.wait_ge(T.sem.loc, loc[0])
    for q in ("v", "t", "s", "g"):
        need("g", (q, n[q]))
    if own:
        g.wait_ge(T.sem.sy, 32)


def _merge(g, core, T, topo, plan, r, c):
    need, did, ts, tt, cp, fill, act, mm, n = [c[k] for k in ("need", "did", "ts", "tt", "cp", "fill", "act", "mm", "n")]
    pi, pf, gf, rf = c["cols"]
    bn, cn = _arrivals(plan, T.cores, topo, r)
    fill(T.fw[:, ZC:FWW], 0.0)
    ts(T.gi[:, 0:1], pi, 4, Op.arith_shift_right)
    t = ts(T.ri[:, 0:1], pi, 15, Op.bitwise_and)
    ts(T.idm[:, :], T.prow[:, :], pf, Op.is_equal)
    need("v", t)
    cp(gf, T.gi[:, 0:1])
    t = cp(rf, T.ri[:, 0:1])
    need("v", t, c["G_g"], c["G_kk"], c["G_nm"])
    ts(T.tri0[:, :], T.prow[:, 0:64], pf, Op.is_ge)
    t = ts(T.tri1[:, :], T.grow[:, :], gf, Op.is_equal)
    ts(T.sel[:, 0:EL], T.prow[:, 0:EL], gf, Op.is_equal)
    ts(T.kq[:, :], T.kk[:, :], 0.0, Op.mult, rf, Op.add)
    need("v", t)
    V_con = tt(T.tri[:, :], T.tri0[:, :], T.tri1[:, :], Op.mult)
    need("t", V_con, c["V_one"])
    mm(T.po[:, 0:60], T.idm[:, :], T.kk[:, :], True, False)

    d = plan[r]["rack"].index(r)
    g.vector.wait_ge(T.sem.cnt, cn)
    for e in range(EL):
        t = cp(T.cc[:, 16 * e:16 * e + 16], T.craw[:, EL * d + e::NE])
    need("t", t)
    t = mm(T.pc[0:64, 0:1], T.cc[:, :], T.ones[:, 0:1], True, True)
    need("v", t)
    t = cp(T.cb[0:64, 0:1], T.pc[0:64, 0:1])
    ts(T.nc[0:64, 0:1], T.pc[0:64, 0:1], -1.0, Op.mult, 256.0, Op.add)
    need("t", t)
    t = mm(T.pb[0:64, 0:1], T.tri[0:64, :], T.cb[0:64, 0:1], True, True)
    need("v", t)
    t = ts(T.bm[0:64, 0:NM], T.nm[0:64, 0:NM], T.pb[0:64, 0:1], Op.add)
    need("v", t)
    for m in range(NM):
        w = T.ind[0:64, 128 * m:128 * m + 128]
        t = ts(w, T.qrow[0:64, :], T.bm[0:64, m:m + 1], Op.is_ge, T.nc[0:64, 0:1], Op.mult)
        need("t", t)
        mm(T.po[:, m:60:NM], w, T.sel[0:64, 0:EL], False, False)
    t = mm(T.po[:, 0:60], T.idm[:, :], T.kq[:, :], False, True)
    need("v", t)
    V_l = cp(T.offf[:, :], T.po[:, 0:60])
    need("v", V_l, ("s", n["s"]))
    need("s", V_l, ("s", n["s"]))
    for q in (g.vector, g.scalar):
        q.wait_ge(T.sem["bin"], bn)
    V_y = cp(T.yt[:, 0:480], T.fw[:, :].indirect(T.offf[:, 0:30]))
    S_y = act(T.yt[:, 480:960], T.fw[:, :].indirect(T.offf[:, 30:60]))
    need("y", V_y)
    g.sync.dma_start(T.y[:, 0:480], T.yt[:, 0:480]).then_inc(T.sem.sy, 16)
    need("s", S_y)
    g.scalar.dma_start(T.y[:, 480:960], T.yt[:, 480:960]).then_inc(T.sem.sy, 16)
